import numpy as np
import ml_dtypes


def mxq(x, axis, fmt="e4m3"):
    dtype, down = {"e4m3": (ml_dtypes.float8_e4m3fn, 7), "e5m2": (ml_dtypes.float8_e5m2, 14)}[fmt]
    v = np.moveaxis(np.asarray(x, np.float32).astype(ml_dtypes.bfloat16).astype(np.float64), axis, -1)
    blocks = v.reshape(v.shape[:-1] + (-1, 32))
    amax = np.abs(blocks).max(-1, keepdims=True)
    byte = np.maximum(np.where(amax > 0, np.frexp(amax)[1] - 1 + 127, 0) - down, 1)
    scale = np.exp2(byte - 127.0)
    codes = (blocks / scale).astype(np.float32).astype(dtype).astype(np.float64)
    return np.moveaxis((codes * scale).reshape(v.shape), -1, axis)


WIDE = False


def mx_kscale(k):
    if not WIDE:
        return np.ones(k)
    levels = np.array([10, -10, 5, -5, 0])
    if k % 512:
        return np.exp2(np.random.permutation(np.resize(levels, k // 32))).repeat(32)
    a = np.empty((k // 512, 16))
    for p in range(k // 512):
        a[p, :8] = np.random.permutation(np.resize(levels, 8))
        for g in range(8):
            far = levels[np.abs(levels - a[p, g]) >= 10]
            a[p, g + 8] = far[np.random.randint(len(far))]
    return np.exp2(a.ravel()).repeat(32)


def f64(x):
    return np.asarray(x).astype(np.float64)


def striped(idx):
    return np.tile(np.asarray(idx).reshape(-1, 16).T, (8, 1)).astype(np.uint16)


def unstriped(offs):
    return offs[:16].T.reshape(-1).astype(np.int64)


E2M1 = np.array([0.0, 0.5, 1.0, 1.5, 2.0, 3.0, 4.0, 6.0, -0.0, -0.5, -1.0, -1.5, -2.0, -3.0, -4.0, -6.0])


def pack_weight(w, fmt):
    k, n = w.shape
    w = f64(np.asarray(w, np.float32).astype(ml_dtypes.bfloat16)).reshape(k // 32, 32, n)
    amax = np.abs(w).max(1)
    if fmt == "e4m3":
        byte = np.frexp(amax)[1] - 1 + 127 - 7
    else:
        mant, ex = np.frexp(amax / 6.0)
        byte = np.where(mant > 0.5, ex, ex - 1) + 127
    byte = np.clip(np.where(amax > 0, byte, 1), 1, 254)
    scaled = (w * np.exp2(127.0 - byte)[:, None, :]).reshape(k, n).astype(np.float32)
    by_word = np.ascontiguousarray(scaled.reshape(k // 512, 128, 4, n).transpose(0, 1, 3, 2))
    if fmt == "e4m3":
        words = by_word.astype(ml_dtypes.float8_e4m3fn).view(np.uint8)
    else:
        c = by_word.astype(ml_dtypes.float4_e2m1fn).view(np.uint8) & 0xF
        words = (c[..., 0::2] | (c[..., 1::2] << 4)).reshape(k // 512, 128, 2 * n)
    return np.ascontiguousarray(words), np.ascontiguousarray(byte.astype(np.uint8).reshape(k // 512, 16, n))


def unpack_weight(words, scales, fmt):
    g, _, n = scales.shape
    words = np.ascontiguousarray(words).reshape(g, 128, n, -1)
    if fmt == "e4m3":
        vals = words.view(ml_dtypes.float8_e4m3fn).astype(np.float64)
    else:
        nib = np.empty((g, 128, n, 4), np.uint8)
        nib[..., 0::2] = words & 0xF
        nib[..., 1::2] = words >> 4
        vals = E2M1[nib]
    vals = vals * np.repeat(np.exp2(scales.astype(np.float64) - 127.0), 8, axis=1)[..., None]
    return vals.transpose(0, 1, 3, 2).reshape(g * 512, n)


B, N, T, D, DV, NQ = 1, 1536, 4096, 512, 256, 256
PAGE = 512


def setup_inputs():
    n = np.random.standard_normal
    pages = np.random.permutation(T // PAGE)[:B * N // PAGE]
    idx = (pages[:, None] * PAGE + np.arange(PAGE)[None, :]).reshape(-1)
    s = mx_kscale(D)[:, None]
    u = np.ones(T)
    u[idx] = mx_kscale(B * N)
    r = np.random.uniform(0.5, 2.0, T)
    qp = [pack_weight(x, "e4m3") for x in n((B, D, NQ)) * s * (0.80 / np.sqrt(D))]
    k = n((D, T)) / s
    v = n((DV, T)) / (u * r)
    kp = pack_weight(k, "e4m3")
    vp = pack_weight(v.T, "e4m3")
    return {
        "q_words": np.stack([x[0] for x in qp]),
        "q_scales": np.stack([x[1] for x in qp]),
        "k_words": kp[0],
        "k_scales": kp[1],
        "v_words": vp[0],
        "v_scales": vp[1],
        "vs": np.tile(u * r, (128, 1)).astype(np.float32),
        "offs": striped(idx),
        "voffs": striped((pages[:, None] * DV + np.arange(DV)[None, :]).reshape(-1)),
    }


def reference(q_words, q_scales, k_words, k_scales, v_words, v_scales, vs, offs, voffs):
    idx = unstriped(offs)
    k = unpack_weight(k_words, k_scales, "e4m3")
    v = unpack_weight(v_words, v_scales, "e4m3")
    v = v.reshape(T // 512, 512, DV)[unstriped(voffs)[::DV] // DV].reshape(B, N, DV)
    pick = lambda x: x[:, idx].reshape(x.shape[0], B, N).transpose(1, 0, 2)
    q = np.stack([unpack_weight(q_words[b], q_scales[b], "e4m3") for b in range(B)])
    score = q.transpose(0, 2, 1) @ pick(k)
    p = 1.0 / (1.0 + np.exp(-score))
    w = p * pick(f64(vs))[:, :1, :]
    y = mxq(w, 2, "e4m3") @ v
    y = y / 16.0
    return y

@@ -1,0 +1,148 @@
+from contextlib import ExitStack
+
+import concourse.mybir as mybir
+from concourse.masks import make_identity
+
+N, T, D, DV, NQ, PAGE = 1536, 4096, 512, 256, 256, 512
+P = 128
+PAGES = N // PAGE
+POOL_PAGES = T // PAGE
+QB = NQ // P
+FLOPS = 2 * NQ * N * (D + DV)
+
+F32 = mybir.dt.float32
+BF16 = mybir.dt.bfloat16
+I32 = mybir.dt.int32
+U32 = mybir.dt.uint32
+U16 = mybir.dt.uint16
+U8 = mybir.dt.uint8
+X4 = mybir.dt.float8_e4m3fn_x4
+ACT = mybir.ActivationFunctionType
+MULT = mybir.AluOpType.mult
+
+V_ROW = 4
+VS_ROW = 16
+
+
+def tile_attend_pkv8q_sigm_kernel(
+    tc, q_words, q_scales, k_words, k_scales, v_words, v_scales, vs, offs, voffs, out
+):
+    nc = tc.nc
+    with ExitStack() as ctx:
+        held = ctx.enter_context(tc.tile_pool(name="held", bufs=1))
+        ring = ctx.enter_context(tc.tile_pool(name="ring", bufs=3))
+        psum = ctx.enter_context(tc.psum_pool(name="psum", bufs=1))
+
+        offs_t = held.tile([P, N // 16], U16, name="offs_t")
+        voffs_t = held.tile([P, PAGES * DV // 16], U16, name="voffs_t")
+        kw_pool = held.tile([P, T], I32, name="kw_pool", align_bytes=64)
+        ks_pool = held.tile([P, T], U8, name="ks_pool", align_bytes=64)
+        vw_pool = held.tile([P, POOL_PAGES, DV], I32, name="vw_pool", align_bytes=64)
+        vb_pool = held.tile([P, POOL_PAGES, DV], U8, name="vb_pool", align_bytes=64)
+        vs_pool = held.tile([P, T], F32, name="vs_pool", align_bytes=64)
+        qw = held.tile([P, NQ], I32, name="qw", align_bytes=64)
+        qs = held.tile([P, NQ], U8, name="qs", align_bytes=64)
+        ident = held.tile([P, P], F32, name="ident", align_bytes=64)
+        warm = held.tile([P, 8], F32, name="warm")
+
+        def replicated(rows16, quad):
+            rows = rows16[4 * quad : 4 * quad + 4, :].bitcast(I32)
+            return rows.unsqueeze(0).broadcast_to([8, 4, rows.shape[1]])
+
+        nc.vector.memset(vs_pool[:], 0.0)
+        nc.gpsimd.memset(warm[:], 0.0)
+        nc.gpsimd.memset(ident[:], 0.0)
+        nc.gpsimd.memset(vb_pool[:].rearrange("p u e -> p (u e)").bitcast(I32), 0)
+        make_identity(nc, ident[:], nomemset=True)
+        nc.scalar.activation(warm[:, 0:1], warm[:, 4:5], ACT.Sigmoid)
+
+        nc.sync.dma_start(offs_t[:], offs)
+        for quad in range(4):
+            nc.sync.dma_start(ks_pool[32 * quad : 32 * quad + 32, :].bitcast(I32), replicated(k_scales[0], quad))
+        nc.sync.dma_start(voffs_t[:], voffs)
+        nc.sync.dma_start(kw_pool[:], k_words[0].rearrange("p n t -> p (n t)").bitcast(I32))
+        nc.sync.dma_start(qw[:], q_words[0, 0].rearrange("p n t -> p (n t)").bitcast(I32))
+        nc.scalar.dma_start(vs_pool[VS_ROW : VS_ROW + 1, :], vs[0:1, :])
+        for quad in range(4):
+            nc.sync.dma_start(qs[32 * quad : 32 * quad + 32, :].bitcast(I32), replicated(q_scales[0, 0], quad))
+        nc.sync.dma_start(vw_pool[:], v_words.rearrange("u p e t -> p u (e t)").bitcast(I32))
+        for quad in range(4):
+            row = 32 * quad + V_ROW
+            nc.gpsimd.dma_start(
+                vb_pool[row : row + 4].bitcast(I32),
+                v_scales[:, 4 * quad : 4 * quad + 4, :].rearrange("u f e -> f u e").bitcast(I32),
+            )
+
+        cols = PAGE // 16
+        ks_g = held.tile([P, N], U8, name="ks_g", align_bytes=64)
+        ks_t = held.tile([P, PAGES, 4, P], U8, name="ks_t", align_bytes=64)
+        nc.vector.tensor_copy(ks_g[:], ks_pool[:].indirect(offs_t[:]))
+        vs_g = held.tile([P, PAGES, PAGE], F32, name="vs_g", align_bytes=64)
+        vs_t = held.tile([P, PAGES, 8], F32, name="vs_t", align_bytes=64)
+        for u in range(PAGES):
+            nc.vector.tensor_copy(vs_g[:, u, :], vs_pool[:].indirect(offs_t[:, u * cols : (u + 1) * cols]))
+            if u == 0:
+                nc.vector.tensor_copy(ks_t[:], ks_g[:].rearrange("p (u m t) -> p u t m", u=PAGES, t=4))
+            turned = psum.tile([P, 4, P], F32, name="turned", bufs=2)
+            for t in range(4):
+                nc.tensor.transpose(turned[:, t, :], vs_g[:, u, t:PAGE:4], ident[:])
+            nc.scalar.copy(vs_t[:, u, 0:4], turned[:, :, VS_ROW])
+
+        kw_g = held.tile([P, PAGES, 4, P], U32, name="kw_g", align_bytes=64)
+        for u in range(PAGES):
+            nc.vector.tensor_copy(
+                kw_g[:, u].rearrange("p t m -> p m t"),
+                kw_pool[:].bitcast(U32).indirect(offs_t[:, u * cols : (u + 1) * cols]),
+            )
+        vb_g = held.tile([P, PAGES * DV], U8, name="vb_g", align_bytes=64)
+        vw_g = held.tile([P, PAGES * DV], U32, name="vw_g", align_bytes=64)
+        nc.vector.tensor_copy(vb_g[:], vb_pool[:].rearrange("p u e -> p (u e)").indirect(voffs_t[:]))
+        nc.vector.tensor_copy(vw_g[:], vw_pool[:].rearrange("p u e -> p (u e)").bitcast(U32).indirect(voffs_t[:]))
+
+        steps = [(b, u) for b in range(QB) for u in range(PAGES)]
+        probs = {}
+        for b, u in steps:
+            score = psum.tile([P, 4, P], F32, name="score", bufs=4)
+            qcols = slice(b * P, (b + 1) * P)
+            for t in range(4):
+                nc.tensor.matmul_mx(
+                    score[:, t, :],
+                    lhsT=kw_g[:, u, t, :].bitcast(X4), lhsT_scale=ks_t[:, u, t, :],
+                    rhs=qw[:, qcols].bitcast(X4), rhs_scale=qs[:, qcols],
+                    start=True, stop=True,
+                )
+            prob = ring.tile([P, P, 4], F32, name="prob", bufs=6)
+            nc.scalar.activation(prob[:], score[:].rearrange("p t q -> p q t"), ACT.Sigmoid)
+            probs[(b, u)] = prob
+
+        weights = {}
+        acc = {}
+
+        def weigh(b, u):
+            w = ring.tile([P, P, 4], BF16, name="w", bufs=6, align_bytes=64)
+            nc.vector.tensor_tensor(w[:], probs[(b, u)][:], vs_t[:, u, 0:4].unsqueeze(1).broadcast_to([P, P, 4]), MULT)
+            weights[(b, u)] = w
+
+        def finish(b, u):
+            codes = ring.tile([P, P], U32, name="codes", bufs=6, align_bytes=64)
+            plane = ring.tile([P, P], U8, name="plane", bufs=6, align_bytes=64)
+            nc.vector.quantize_mx(codes[:].bitcast(X4), plane[:], weights[(b, u)][:].rearrange("p q t -> p (q t)"))
+            if u == 0:
+                acc[b] = psum.tile([P, DV], F32, name="acc", bufs=2)
+            ecols = slice(u * DV, (u + 1) * DV)
+            nc.tensor.matmul_mx(
+                acc[b][:],
+                lhsT=codes[:].bitcast(X4), lhsT_scale=plane[:],
+                rhs=vw_g[:, ecols].bitcast(X4), rhs_scale=vb_g[V_ROW:P, ecols],
+                start=(u == 0), stop=(u == PAGES - 1),
+            )
+            if u == PAGES - 1:
+                res = ring.tile([P, DV], F32, name="res", bufs=2)
+                nc.scalar.activation(res[:], acc[b][:], ACT.Copy, scale=1.0 / 16.0)
+                nc.sync.dma_start(out[0, b * P : (b + 1) * P, :], res[:])
+
+        weigh(*steps[0])
+        for i in range(1, len(steps)):
+            weigh(*steps[i])
+            finish(*steps[i - 1])
+        finish(*steps[-1])

@@ -21,7 +21,7 @@ ACT = mybir.ActivationFunctionType
 MULT = mybir.AluOpType.mult
 
 V_ROW = 4
-VS_ROW = 16
+VS_ROW = 127
 
 
 def tile_attend_pkv8q_sigm_kernel(
@@ -49,7 +49,8 @@ def tile_attend_pkv8q_sigm_kernel(
             rows = rows16[4 * quad : 4 * quad + 4, :].bitcast(I32)
             return rows.unsqueeze(0).broadcast_to([8, 4, rows.shape[1]])
 
-        nc.vector.memset(vs_pool[:], 0.0)
+        nc.scalar.dma_start(vs_pool[VS_ROW : VS_ROW + 1, :], vs[0:1, :])
+        nc.vector.memset(vs_pool[0:VS_ROW, :], 0.0)
         nc.gpsimd.memset(warm[:], 0.0)
         nc.gpsimd.memset(ident[:], 0.0)
         nc.gpsimd.memset(vb_pool[:].rearrange("p u e -> p (u e)").bitcast(I32), 0)
@@ -62,7 +63,6 @@ def tile_attend_pkv8q_sigm_kernel(
         nc.sync.dma_start(voffs_t[:], voffs)
         nc.sync.dma_start(kw_pool[:], k_words[0].rearrange("p n t -> p (n t)").bitcast(I32))
         nc.sync.dma_start(qw[:], q_words[0, 0].rearrange("p n t -> p (n t)").bitcast(I32))
-        nc.scalar.dma_start(vs_pool[VS_ROW : VS_ROW + 1, :], vs[0:1, :])
         for quad in range(4):
             nc.sync.dma_start(qs[32 * quad : 32 * quad + 32, :].bitcast(I32), replicated(q_scales[0, 0], quad))
         nc.sync.dma_start(vw_pool[:], v_words.rearrange("u p e t -> p u (e t)").bitcast(I32))
@@ -76,19 +76,18 @@ def tile_attend_pkv8q_sigm_kernel(
         cols = PAGE // 16
         ks_g = held.tile([P, N], U8, name="ks_g", align_bytes=64)
         ks_t = held.tile([P, PAGES, 4, P], U8, name="ks_t", align_bytes=64)
-        nc.vector.tensor_copy(ks_g[:], ks_pool[:].indirect(offs_t[:]))
         vs_g = held.tile([P, PAGES, PAGE], F32, name="vs_g", align_bytes=64)
         vs_t = held.tile([P, PAGES, 8], F32, name="vs_t", align_bytes=64)
         for u in range(PAGES):
             nc.vector.tensor_copy(vs_g[:, u, :], vs_pool[:].indirect(offs_t[:, u * cols : (u + 1) * cols]))
-            if u == 0:
-                nc.vector.tensor_copy(ks_t[:], ks_g[:].rearrange("p (u m t) -> p u t m", u=PAGES, t=4))
             turned = psum.tile([P, 4, P], F32, name="turned", bufs=2)
             for t in range(4):
                 nc.tensor.transpose(turned[:, t, :], vs_g[:, u, t:PAGE:4], ident[:])
             nc.scalar.copy(vs_t[:, u, 0:4], turned[:, :, VS_ROW])
 
         kw_g = held.tile([P, PAGES, 4, P], U32, name="kw_g", align_bytes=64)
+        nc.vector.tensor_copy(ks_g[:], ks_pool[:].indirect(offs_t[:]))
+        nc.vector.tensor_copy(ks_t[:], ks_g[:].rearrange("p (u m t) -> p u t m", u=PAGES, t=4))
         for u in range(PAGES):
             nc.vector.tensor_copy(
                 kw_g[:, u].rearrange("p t m -> p m t"),

@@ -78,16 +78,20 @@ def tile_attend_pkv8q_sigm_kernel(
         ks_t = held.tile([P, PAGES, 4, P], U8, name="ks_t", align_bytes=64)
         vs_g = held.tile([P, PAGES, PAGE], F32, name="vs_g", align_bytes=64)
         vs_t = held.tile([P, PAGES, 8], F32, name="vs_t", align_bytes=64)
+        nc.vector.tensor_copy(vs_g[:].rearrange("p u j -> p (u j)"), vs_pool[:].indirect(offs_t[:]))
         for u in range(PAGES):
-            nc.vector.tensor_copy(vs_g[:, u, :], vs_pool[:].indirect(offs_t[:, u * cols : (u + 1) * cols]))
             turned = psum.tile([P, 4, P], F32, name="turned", bufs=2)
             for t in range(4):
                 nc.tensor.transpose(turned[:, t, :], vs_g[:, u, t:PAGE:4], ident[:])
             nc.scalar.copy(vs_t[:, u, 0:4], turned[:, :, VS_ROW])
 
         kw_g = held.tile([P, PAGES, 4, P], U32, name="kw_g", align_bytes=64)
-        nc.vector.tensor_copy(ks_g[:], ks_pool[:].indirect(offs_t[:]))
-        nc.vector.tensor_copy(ks_t[:], ks_g[:].rearrange("p (u m t) -> p u t m", u=PAGES, t=4))
+        for lo, hi in ((0, PAGES - 1), (PAGES - 1, PAGES)):
+            nc.vector.tensor_copy(ks_g[:, lo * PAGE : hi * PAGE], ks_pool[:].indirect(offs_t[:, lo * cols : hi * cols]))
+        for lo, hi in ((0, PAGES - 1), (PAGES - 1, PAGES)):
+            nc.vector.tensor_copy(
+                ks_t[:, lo:hi], ks_g[:, lo * PAGE : hi * PAGE].rearrange("p (u m t) -> p u t m", u=hi - lo, t=4)
+            )
         for u in range(PAGES):
             nc.vector.tensor_copy(
                 kw_g[:, u].rearrange("p t m -> p m t"),

@@ -21,7 +21,7 @@ ACT = mybir.ActivationFunctionType
 MULT = mybir.AluOpType.mult
 
 V_ROW = 4
-VS_ROW = 127
+VS_ROW = P - POOL_PAGES
 
 
 def tile_attend_pkv8q_sigm_kernel(
@@ -30,41 +30,51 @@ def tile_attend_pkv8q_sigm_kernel(
     nc = tc.nc
     with ExitStack() as ctx:
         held = ctx.enter_context(tc.tile_pool(name="held", bufs=1))
+        laid = ctx.enter_context(tc.tile_pool(name="laid", bufs=1))
         ring = ctx.enter_context(tc.tile_pool(name="ring", bufs=3))
         psum = ctx.enter_context(tc.psum_pool(name="psum", bufs=1))
 
         offs_t = held.tile([P, N // 16], U16, name="offs_t")
         voffs_t = held.tile([P, PAGES * DV // 16], U16, name="voffs_t")
-        kw_pool = held.tile([P, T], I32, name="kw_pool", align_bytes=64)
         ks_pool = held.tile([P, T], U8, name="ks_pool", align_bytes=64)
-        vw_pool = held.tile([P, POOL_PAGES, DV], I32, name="vw_pool", align_bytes=64)
-        vb_pool = held.tile([P, POOL_PAGES, DV], U8, name="vb_pool", align_bytes=64)
-        vs_pool = held.tile([P, T], F32, name="vs_pool", align_bytes=64)
-        qw = held.tile([P, NQ], I32, name="qw", align_bytes=64)
-        qs = held.tile([P, NQ], U8, name="qs", align_bytes=64)
+        vs_rows = held.tile([P, PAGE], F32, name="vs_rows", align_bytes=64)
+        vs_pool = held.tile([P, POOL_PAGES, PAGE], F32, name="vs_pool", align_bytes=64)
         ident = held.tile([P, P], F32, name="ident", align_bytes=64)
-        warm = held.tile([P, 8], F32, name="warm")
+        warm = held.tile([P, 32], F32, name="warm")
 
-        def replicated(rows16, quad):
-            rows = rows16[4 * quad : 4 * quad + 4, :].bitcast(I32)
-            return rows.unsqueeze(0).broadcast_to([8, 4, rows.shape[1]])
-
-        nc.scalar.dma_start(vs_pool[VS_ROW : VS_ROW + 1, :], vs[0:1, :])
-        nc.vector.memset(vs_pool[0:VS_ROW, :], 0.0)
-        nc.gpsimd.memset(warm[:], 0.0)
-        nc.gpsimd.memset(ident[:], 0.0)
-        nc.gpsimd.memset(vb_pool[:].rearrange("p u e -> p (u e)").bitcast(I32), 0)
-        make_identity(nc, ident[:], nomemset=True)
-        nc.scalar.activation(warm[:, 0:1], warm[:, 4:5], ACT.Sigmoid)
+        qw_at = 4 * T
+        vw_at = qw_at + 4 * NQ
+        vb_at = vw_at + 4 * POOL_PAGES * DV
+        vb_pool = laid.tile([P, POOL_PAGES, DV], U8, name="vb_pool", align_bytes=64, offset=vb_at)
+        kw_pool = laid.tile([P, T], I32, name="kw_pool", align_bytes=64, offset=0)
+        zeros = laid.tile([P, 32], F32, name="zeros", align_bytes=64, offset=vw_at - 64)
 
         nc.sync.dma_start(offs_t[:], offs)
-        for quad in range(4):
-            nc.sync.dma_start(ks_pool[32 * quad : 32 * quad + 32, :].bitcast(I32), replicated(k_scales[0], quad))
+        nc.sync.dma_start(vs_rows[VS_ROW:P, :], vs[0, :].rearrange("(u j) -> u j", j=PAGE))
         nc.sync.dma_start(voffs_t[:], voffs)
         nc.sync.dma_start(kw_pool[:], k_words[0].rearrange("p n t -> p (n t)").bitcast(I32))
-        nc.sync.dma_start(qw[:], q_words[0, 0].rearrange("p n t -> p (n t)").bitcast(I32))
+
+        qs = held.tile([P, NQ], U8, name="qs", align_bytes=64)
         for quad in range(4):
-            nc.sync.dma_start(qs[32 * quad : 32 * quad + 32, :].bitcast(I32), replicated(q_scales[0, 0], quad))
+            rows = q_scales[0, 0, 4 * quad : 4 * quad + 4, :].bitcast(I32)
+            nc.scalar.dma_start(
+                qs[32 * quad : 32 * quad + 32, :].bitcast(I32), rows.unsqueeze(0).broadcast_to([8, 4, NQ // 4])
+            )
+
+        nc.gpsimd.memset(ident[:], 0.0)
+        make_identity(nc, ident[:], nomemset=True)
+        nc.vector.memset(ks_pool[:].bitcast(I32), 0)
+        nc.vector.memset(zeros[:], 0.0)
+        nc.vector.memset(vs_rows[0:VS_ROW, :], 0.0)
+        nc.vector.memset(vb_pool[:].rearrange("p u e -> p (u e)").bitcast(I32), 0)
+        nc.vector.memset(vs_pool[:].rearrange("p u j -> p (u j)"), 0.0)
+        for r in range(4):
+            nc.scalar.dma_start(ks_pool[r:P:32, :].bitcast(I32), k_scales[0, r:16:4, :].bitcast(I32))
+        nc.scalar.activation(warm[:], zeros[:], ACT.Sigmoid)
+
+        qw = laid.tile([P, NQ], I32, name="qw", align_bytes=64, offset=qw_at)
+        vw_pool = laid.tile([P, POOL_PAGES, DV], I32, name="vw_pool", align_bytes=64, offset=vw_at)
+        nc.sync.dma_start(qw[:], q_words[0, 0].rearrange("p n t -> p (n t)").bitcast(I32))
         nc.sync.dma_start(vw_pool[:], v_words.rearrange("u p e t -> p u (e t)").bitcast(I32))
         for quad in range(4):
             row = 32 * quad + V_ROW
@@ -73,18 +83,15 @@ def tile_attend_pkv8q_sigm_kernel(
                 v_scales[:, 4 * quad : 4 * quad + 4, :].rearrange("u f e -> f u e").bitcast(I32),
             )
 
+        turned = psum.tile([P, 4, P], F32, name="turned")
+        for t in range(4):
+            nc.tensor.transpose(turned[:, t, :], vs_rows[:, t:PAGE:4], ident[:])
+        nc.scalar.copy(vs_pool[:, :, 0:4], turned[:, :, VS_ROW:P].rearrange("p t u -> p u t"))
+
         cols = PAGE // 16
         ks_g = held.tile([P, N], U8, name="ks_g", align_bytes=64)
         ks_t = held.tile([P, PAGES, 4, P], U8, name="ks_t", align_bytes=64)
         vs_g = held.tile([P, PAGES, PAGE], F32, name="vs_g", align_bytes=64)
-        vs_t = held.tile([P, PAGES, 8], F32, name="vs_t", align_bytes=64)
-        nc.vector.tensor_copy(vs_g[:].rearrange("p u j -> p (u j)"), vs_pool[:].indirect(offs_t[:]))
-        for u in range(PAGES):
-            turned = psum.tile([P, 4, P], F32, name="turned", bufs=2)
-            for t in range(4):
-                nc.tensor.transpose(turned[:, t, :], vs_g[:, u, t:PAGE:4], ident[:])
-            nc.scalar.copy(vs_t[:, u, 0:4], turned[:, :, VS_ROW])
-
         kw_g = held.tile([P, PAGES, 4, P], U32, name="kw_g", align_bytes=64)
         for lo, hi in ((0, PAGES - 1), (PAGES - 1, PAGES)):
             nc.vector.tensor_copy(ks_g[:, lo * PAGE : hi * PAGE], ks_pool[:].indirect(offs_t[:, lo * cols : hi * cols]))
@@ -92,17 +99,18 @@ def tile_attend_pkv8q_sigm_kernel(
             nc.vector.tensor_copy(
                 ks_t[:, lo:hi], ks_g[:, lo * PAGE : hi * PAGE].rearrange("p (u m t) -> p u t m", u=hi - lo, t=4)
             )
+        nc.vector.tensor_copy(
+            vs_g[:].rearrange("p u j -> p (u j)"), vs_pool[:].rearrange("p u j -> p (u j)").indirect(offs_t[:])
+        )
         for u in range(PAGES):
             nc.vector.tensor_copy(
                 kw_g[:, u].rearrange("p t m -> p m t"),
                 kw_pool[:].bitcast(U32).indirect(offs_t[:, u * cols : (u + 1) * cols]),
             )
-        vb_g = held.tile([P, PAGES * DV], U8, name="vb_g", align_bytes=64)
-        vw_g = held.tile([P, PAGES * DV], U32, name="vw_g", align_bytes=64)
-        nc.vector.tensor_copy(vb_g[:], vb_pool[:].rearrange("p u e -> p (u e)").indirect(voffs_t[:]))
-        nc.vector.tensor_copy(vw_g[:], vw_pool[:].rearrange("p u e -> p (u e)").bitcast(U32).indirect(voffs_t[:]))
+        vb_g = laid.tile([P, PAGES * DV], U8, name="vb_g", align_bytes=64, offset=0)
+        vw_g = laid.tile([P, PAGES * DV], U32, name="vw_g", align_bytes=64, offset=PAGES * DV)
 
-        steps = [(b, u) for b in range(QB) for u in range(PAGES)]
+        steps = [(b, u) for u in range(PAGES) for b in range(QB)]
         probs = {}
         for b, u in steps:
             score = psum.tile([P, 4, P], F32, name="score", bufs=4)
@@ -122,8 +130,11 @@ def tile_attend_pkv8q_sigm_kernel(
         acc = {}
 
         def weigh(b, u):
-            w = ring.tile([P, P, 4], BF16, name="w", bufs=6, align_bytes=64)
-            nc.vector.tensor_tensor(w[:], probs[(b, u)][:], vs_t[:, u, 0:4].unsqueeze(1).broadcast_to([P, P, 4]), MULT)
+            if u == 1:
+                w = laid.tile([P, P, 4], BF16, name="w1%d" % b, align_bytes=64, offset=(vb_at, vw_at)[b])
+            else:
+                w = ring.tile([P, P, 4], BF16, name="w", bufs=4, align_bytes=64)
+            nc.vector.tensor_tensor(w[:], probs[(b, u)][:], vs_g[:, u, 0:4].unsqueeze(1).broadcast_to([P, P, 4]), MULT)
             weights[(b, u)] = w
 
         def finish(b, u):
@@ -144,8 +155,12 @@ def tile_attend_pkv8q_sigm_kernel(
                 nc.scalar.activation(res[:], acc[b][:], ACT.Copy, scale=1.0 / 16.0)
                 nc.sync.dma_start(out[0, b * P : (b + 1) * P, :], res[:])
 
+        nc.vector.tensor_copy(vb_g[:], vb_pool[:].rearrange("p u e -> p (u e)").indirect(voffs_t[:]))
         weigh(*steps[0])
-        for i in range(1, len(steps)):
+        weigh(*steps[1])
+        nc.vector.tensor_copy(vw_g[:], vw_pool[:].rearrange("p u e -> p (u e)").bitcast(U32).indirect(voffs_t[:]))
+        finish(*steps[0])
+        for i in range(2, len(steps)):
             weigh(*steps[i])
             finish(*steps[i - 1])
         finish(*steps[-1])

@@ -21,7 +21,8 @@ ACT = mybir.ActivationFunctionType
 MULT = mybir.AluOpType.mult
 
 V_ROW = 4
-VS_ROW = P - POOL_PAGES
+VS_ROW = P - 1
+K_HEAD = T // 4
 
 
 def tile_attend_pkv8q_sigm_kernel(
@@ -37,44 +38,40 @@ def tile_attend_pkv8q_sigm_kernel(
         offs_t = held.tile([P, N // 16], U16, name="offs_t")
         voffs_t = held.tile([P, PAGES * DV // 16], U16, name="voffs_t")
         ks_pool = held.tile([P, T], U8, name="ks_pool", align_bytes=64)
-        vs_rows = held.tile([P, PAGE], F32, name="vs_rows", align_bytes=64)
-        vs_pool = held.tile([P, POOL_PAGES, PAGE], F32, name="vs_pool", align_bytes=64)
+        vs_pool = held.tile([P, T], F32, name="vs_pool", align_bytes=64)
         ident = held.tile([P, P], F32, name="ident", align_bytes=64)
-        warm = held.tile([P, 32], F32, name="warm")
+        warm = held.tile([P, 8], F32, name="warm")
 
-        qw_at = 4 * T
-        vw_at = qw_at + 4 * NQ
-        vb_at = vw_at + 4 * POOL_PAGES * DV
-        vb_pool = laid.tile([P, POOL_PAGES, DV], U8, name="vb_pool", align_bytes=64, offset=vb_at)
-        kw_pool = laid.tile([P, T], I32, name="kw_pool", align_bytes=64, offset=0)
-        zeros = laid.tile([P, 32], F32, name="zeros", align_bytes=64, offset=vw_at - 64)
-
-        nc.sync.dma_start(offs_t[:], offs)
-        nc.sync.dma_start(vs_rows[VS_ROW:P, :], vs[0, :].rearrange("(u j) -> u j", j=PAGE))
-        nc.sync.dma_start(voffs_t[:], voffs)
-        nc.sync.dma_start(kw_pool[:], k_words[0].rearrange("p n t -> p (n t)").bitcast(I32))
-
+        qw = held.tile([P, NQ], I32, name="qw", align_bytes=64)
         qs = held.tile([P, NQ], U8, name="qs", align_bytes=64)
-        for quad in range(4):
-            rows = q_scales[0, 0, 4 * quad : 4 * quad + 4, :].bitcast(I32)
-            nc.scalar.dma_start(
-                qs[32 * quad : 32 * quad + 32, :].bitcast(I32), rows.unsqueeze(0).broadcast_to([8, 4, NQ // 4])
-            )
+        vw_at = 4 * T
+        vb_at = vw_at + 4 * POOL_PAGES * DV
+        kw_pool = laid.tile([P, T], I32, name="kw_pool", align_bytes=64, offset=0)
+        vw_pool = laid.tile([P, POOL_PAGES, DV], I32, name="vw_pool", align_bytes=64, offset=vw_at)
+        vb_pool = laid.tile([P, POOL_PAGES, DV], U8, name="vb_pool", align_bytes=64, offset=vb_at)
 
+        nc.gpsimd.memset(ks_pool[:].bitcast(I32), 0)
+        nc.gpsimd.memset(warm[:], 0.0)
         nc.gpsimd.memset(ident[:], 0.0)
         make_identity(nc, ident[:], nomemset=True)
-        nc.vector.memset(ks_pool[:].bitcast(I32), 0)
-        nc.vector.memset(zeros[:], 0.0)
-        nc.vector.memset(vs_rows[0:VS_ROW, :], 0.0)
-        nc.vector.memset(vb_pool[:].rearrange("p u e -> p (u e)").bitcast(I32), 0)
-        nc.vector.memset(vs_pool[:].rearrange("p u j -> p (u j)"), 0.0)
-        for r in range(4):
-            nc.scalar.dma_start(ks_pool[r:P:32, :].bitcast(I32), k_scales[0, r:16:4, :].bitcast(I32))
-        nc.scalar.activation(warm[:], zeros[:], ACT.Sigmoid)
+        nc.gpsimd.memset(vb_pool[:].rearrange("p u e -> p (u e)").bitcast(I32), 0)
+        nc.vector.memset(vs_pool[0:VS_ROW, :], 0.0)
+        nc.scalar.activation(warm[:, 0:1], warm[:, 4:5], ACT.Sigmoid)
 
-        qw = laid.tile([P, NQ], I32, name="qw", align_bytes=64, offset=qw_at)
-        vw_pool = laid.tile([P, POOL_PAGES, DV], I32, name="vw_pool", align_bytes=64, offset=vw_at)
+        k_flat = k_words[0].rearrange("p n t -> p (n t)").bitcast(I32)
+        nc.sync.dma_start(offs_t[:], offs)
+        nc.sync.dma_start(vs_pool[VS_ROW:P, :], vs[0:1, :])
+        nc.sync.dma_start(kw_pool[:, 0:K_HEAD], k_flat[:, 0:K_HEAD])
+        for r in range(4):
+            nc.sync.dma_start(ks_pool[r:P:32, :].bitcast(I32), k_scales[0, r:16:4, :].bitcast(I32))
+        nc.sync.dma_start(kw_pool[:, K_HEAD:T], k_flat[:, K_HEAD:T])
         nc.sync.dma_start(qw[:], q_words[0, 0].rearrange("p n t -> p (n t)").bitcast(I32))
+        for quad in range(4):
+            rows = q_scales[0, 0, 4 * quad : 4 * quad + 4, :].bitcast(I32)
+            nc.sync.dma_start(
+                qs[32 * quad : 32 * quad + 32, :].bitcast(I32), rows.unsqueeze(0).broadcast_to([8, 4, NQ // 4])
+            )
+        nc.sync.dma_start(voffs_t[:], voffs)
         nc.sync.dma_start(vw_pool[:], v_words.rearrange("u p e t -> p u (e t)").bitcast(I32))
         for quad in range(4):
             row = 32 * quad + V_ROW
@@ -83,25 +80,26 @@ def tile_attend_pkv8q_sigm_kernel(
                 v_scales[:, 4 * quad : 4 * quad + 4, :].rearrange("u f e -> f u e").bitcast(I32),
             )
 
-        turned = psum.tile([P, 4, P], F32, name="turned")
-        for t in range(4):
-            nc.tensor.transpose(turned[:, t, :], vs_rows[:, t:PAGE:4], ident[:])
-        nc.scalar.copy(vs_pool[:, :, 0:4], turned[:, :, VS_ROW:P].rearrange("p t u -> p u t"))
-
         cols = PAGE // 16
         ks_g = held.tile([P, N], U8, name="ks_g", align_bytes=64)
         ks_t = held.tile([P, PAGES, 4, P], U8, name="ks_t", align_bytes=64)
         vs_g = held.tile([P, PAGES, PAGE], F32, name="vs_g", align_bytes=64)
         kw_g = held.tile([P, PAGES, 4, P], U32, name="kw_g", align_bytes=64)
+        vs_d = held.tile([P, PAGES, 4, P], F32, name="vs_d", align_bytes=64)
+        vs_t = held.tile([P, PAGES, 8], F32, name="vs_t", align_bytes=64)
+        nc.vector.tensor_copy(vs_g[:].rearrange("p u j -> p (u j)"), vs_pool[:].indirect(offs_t[:]))
+        for u in range(PAGES):
+            nc.scalar.copy(vs_d[:, u].rearrange("p t m -> p m t"), vs_g[:, u].rearrange("p (m t) -> p m t", t=4))
+            turned = psum.tile([P, 4, P], F32, name="turned", bufs=2)
+            for t in range(4):
+                nc.tensor.transpose(turned[:, t, :], vs_d[:, u, t, :], ident[:])
+            nc.scalar.copy(vs_t[:, u, 0:4], turned[:, :, VS_ROW])
         for lo, hi in ((0, PAGES - 1), (PAGES - 1, PAGES)):
             nc.vector.tensor_copy(ks_g[:, lo * PAGE : hi * PAGE], ks_pool[:].indirect(offs_t[:, lo * cols : hi * cols]))
         for lo, hi in ((0, PAGES - 1), (PAGES - 1, PAGES)):
             nc.vector.tensor_copy(
                 ks_t[:, lo:hi], ks_g[:, lo * PAGE : hi * PAGE].rearrange("p (u m t) -> p u t m", u=hi - lo, t=4)
             )
-        nc.vector.tensor_copy(
-            vs_g[:].rearrange("p u j -> p (u j)"), vs_pool[:].rearrange("p u j -> p (u j)").indirect(offs_t[:])
-        )
         for u in range(PAGES):
             nc.vector.tensor_copy(
                 kw_g[:, u].rearrange("p t m -> p m t"),
@@ -134,7 +132,7 @@ def tile_attend_pkv8q_sigm_kernel(
                 w = laid.tile([P, P, 4], BF16, name="w1%d" % b, align_bytes=64, offset=(vb_at, vw_at)[b])
             else:
                 w = ring.tile([P, P, 4], BF16, name="w", bufs=4, align_bytes=64)
-            nc.vector.tensor_tensor(w[:], probs[(b, u)][:], vs_g[:, u, 0:4].unsqueeze(1).broadcast_to([P, P, 4]), MULT)
+            nc.vector.tensor_tensor(w[:], probs[(b, u)][:], vs_t[:, u, 0:4].unsqueeze(1).broadcast_to([P, P, 4]), MULT)
             weights[(b, u)] = w
 
         def finish(b, u):

@@ -50,12 +50,11 @@ def tile_attend_pkv8q_sigm_kernel(
         vw_pool = laid.tile([P, POOL_PAGES, DV], I32, name="vw_pool", align_bytes=64, offset=vw_at)
         vb_pool = laid.tile([P, POOL_PAGES, DV], U8, name="vb_pool", align_bytes=64, offset=vb_at)
 
-        nc.gpsimd.memset(ks_pool[:].bitcast(I32), 0)
-        nc.gpsimd.memset(warm[:], 0.0)
-        nc.gpsimd.memset(ident[:], 0.0)
-        make_identity(nc, ident[:], nomemset=True)
-        nc.gpsimd.memset(vb_pool[:].rearrange("p u e -> p (u e)").bitcast(I32), 0)
+        make_identity(nc, ident[:])
+        nc.vector.memset(ks_pool[:].bitcast(I32), 0)
+        nc.vector.memset(warm[:], 0.0)
         nc.vector.memset(vs_pool[0:VS_ROW, :], 0.0)
+        nc.vector.memset(vb_pool[:].rearrange("p u e -> p (u e)").bitcast(I32), 0)
         nc.scalar.activation(warm[:, 0:1], warm[:, 4:5], ACT.Sigmoid)
 
         k_flat = k_words[0].rearrange("p n t -> p (n t)").bitcast(I32)
@@ -73,11 +72,10 @@ def tile_attend_pkv8q_sigm_kernel(
             )
         nc.sync.dma_start(voffs_t[:], voffs)
         nc.sync.dma_start(vw_pool[:], v_words.rearrange("u p e t -> p u (e t)").bitcast(I32))
-        for quad in range(4):
-            row = 32 * quad + V_ROW
-            nc.gpsimd.dma_start(
-                vb_pool[row : row + 4].bitcast(I32),
-                v_scales[:, 4 * quad : 4 * quad + 4, :].rearrange("u f e -> f u e").bitcast(I32),
+        for r in range(4):
+            nc.sync.dma_start(
+                vb_pool[V_ROW + r : P : 32].bitcast(I32),
+                v_scales[:, r:16:4, :].rearrange("u f e -> f u e").bitcast(I32),
             )
 
         cols = PAGE // 16
@@ -125,22 +123,26 @@ def tile_attend_pkv8q_sigm_kernel(
             probs[(b, u)] = prob
 
         weights = {}
-        acc = {}
+        packed = {}
+        acc = [psum.tile([P, DV], F32, name="acc%d" % b) for b in range(QB)]
+        behind = {steps[3]: vw_at, steps[4]: vb_at}
 
         def weigh(b, u):
-            if u == 1:
-                w = laid.tile([P, P, 4], BF16, name="w1%d" % b, align_bytes=64, offset=(vb_at, vw_at)[b])
+            if (b, u) in behind:
+                w = laid.tile([P, P, 4], BF16, name="w%d%d" % (b, u), align_bytes=64, offset=behind[(b, u)])
             else:
                 w = ring.tile([P, P, 4], BF16, name="w", bufs=4, align_bytes=64)
             nc.vector.tensor_tensor(w[:], probs[(b, u)][:], vs_t[:, u, 0:4].unsqueeze(1).broadcast_to([P, P, 4]), MULT)
             weights[(b, u)] = w
 
-        def finish(b, u):
+        def quantise(b, u):
             codes = ring.tile([P, P], U32, name="codes", bufs=6, align_bytes=64)
             plane = ring.tile([P, P], U8, name="plane", bufs=6, align_bytes=64)
             nc.vector.quantize_mx(codes[:].bitcast(X4), plane[:], weights[(b, u)][:].rearrange("p q t -> p (q t)"))
-            if u == 0:
-                acc[b] = psum.tile([P, DV], F32, name="acc", bufs=2)
+            packed[(b, u)] = (codes, plane)
+
+        def multiply(b, u):
+            codes, plane = packed[(b, u)]
             ecols = slice(u * DV, (u + 1) * DV)
             nc.tensor.matmul_mx(
                 acc[b][:],
@@ -148,17 +150,21 @@ def tile_attend_pkv8q_sigm_kernel(
                 rhs=vw_g[:, ecols].bitcast(X4), rhs_scale=vb_g[V_ROW:P, ecols],
                 start=(u == 0), stop=(u == PAGES - 1),
             )
-            if u == PAGES - 1:
-                res = ring.tile([P, DV], F32, name="res", bufs=2)
-                nc.scalar.activation(res[:], acc[b][:], ACT.Copy, scale=1.0 / 16.0)
-                nc.sync.dma_start(out[0, b * P : (b + 1) * P, :], res[:])
 
-        nc.vector.tensor_copy(vb_g[:], vb_pool[:].rearrange("p u e -> p (u e)").indirect(voffs_t[:]))
         weigh(*steps[0])
-        weigh(*steps[1])
-        nc.vector.tensor_copy(vw_g[:], vw_pool[:].rearrange("p u e -> p (u e)").bitcast(U32).indirect(voffs_t[:]))
-        finish(*steps[0])
-        for i in range(2, len(steps)):
+        for i in range(1, len(steps)):
+            if i == 3:
+                nc.vector.tensor_copy(
+                    vw_g[:], vw_pool[:].rearrange("p u e -> p (u e)").bitcast(U32).indirect(voffs_t[:])
+                )
+            if i == 4:
+                nc.vector.tensor_copy(vb_g[:], vb_pool[:].rearrange("p u e -> p (u e)").indirect(voffs_t[:]))
             weigh(*steps[i])
-            finish(*steps[i - 1])
-        finish(*steps[-1])
+            quantise(*steps[i - 1])
+        quantise(*steps[-1])
+        for b, u in steps:
+            multiply(b, u)
+        for b in range(QB):
+            res = ring.tile([P, DV], F32, name="res", bufs=2)
+            nc.scalar.activation(res[:], acc[b][:], ACT.Copy, scale=1.0 / 16.0)
+            nc.sync.dma_start(out[0, b * P : (b + 1) * P, :], res[:])

@@ -23,6 +23,7 @@ MULT = mybir.AluOpType.mult
 V_ROW = 4
 VS_ROW = P - 1
 K_HEAD = T // 4
+ON_SCALAR = (0, PAGES - 1)
 
 
 def tile_attend_pkv8q_sigm_kernel(
@@ -44,11 +45,9 @@ def tile_attend_pkv8q_sigm_kernel(
 
         qw = held.tile([P, NQ], I32, name="qw", align_bytes=64)
         qs = held.tile([P, NQ], U8, name="qs", align_bytes=64)
-        vw_at = 4 * T
-        vb_at = vw_at + 4 * POOL_PAGES * DV
-        kw_pool = laid.tile([P, T], I32, name="kw_pool", align_bytes=64, offset=0)
-        vw_pool = laid.tile([P, POOL_PAGES, DV], I32, name="vw_pool", align_bytes=64, offset=vw_at)
-        vb_pool = laid.tile([P, POOL_PAGES, DV], U8, name="vb_pool", align_bytes=64, offset=vb_at)
+        kw_pool = held.tile([P, T], I32, name="kw_pool", align_bytes=64)
+        vw_pool = laid.tile([P, POOL_PAGES, DV], I32, name="vw_pool", align_bytes=64, offset=0)
+        vb_pool = held.tile([P, POOL_PAGES, DV], U8, name="vb_pool", align_bytes=64)
 
         make_identity(nc, ident[:])
         nc.vector.memset(ks_pool[:].bitcast(I32), 0)
@@ -58,25 +57,31 @@ def tile_attend_pkv8q_sigm_kernel(
         nc.scalar.activation(warm[:, 0:1], warm[:, 4:5], ACT.Sigmoid)
 
         k_flat = k_words[0].rearrange("p n t -> p (n t)").bitcast(I32)
-        nc.sync.dma_start(offs_t[:], offs)
-        nc.sync.dma_start(vs_pool[VS_ROW:P, :], vs[0:1, :])
-        nc.sync.dma_start(kw_pool[:, 0:K_HEAD], k_flat[:, 0:K_HEAD])
-        for r in range(4):
-            nc.sync.dma_start(ks_pool[r:P:32, :].bitcast(I32), k_scales[0, r:16:4, :].bitcast(I32))
-        nc.sync.dma_start(kw_pool[:, K_HEAD:T], k_flat[:, K_HEAD:T])
-        nc.sync.dma_start(qw[:], q_words[0, 0].rearrange("p n t -> p (n t)").bitcast(I32))
-        for quad in range(4):
+
+        def load_q_scales(quad):
             rows = q_scales[0, 0, 4 * quad : 4 * quad + 4, :].bitcast(I32)
             nc.sync.dma_start(
                 qs[32 * quad : 32 * quad + 32, :].bitcast(I32), rows.unsqueeze(0).broadcast_to([8, 4, NQ // 4])
             )
+
+        nc.sync.dma_start(offs_t[:], offs)
         nc.sync.dma_start(voffs_t[:], voffs)
-        nc.sync.dma_start(vw_pool[:], v_words.rearrange("u p e t -> p u (e t)").bitcast(I32))
+        nc.sync.dma_start(vs_pool[VS_ROW:P, :], vs[0:1, :])
+        nc.sync.dma_start(kw_pool[:, 0:K_HEAD], k_flat[:, 0:K_HEAD])
+        for r in range(4):
+            nc.sync.dma_start(ks_pool[r:P:32, :].bitcast(I32), k_scales[0, r:16:4, :].bitcast(I32))
+        load_q_scales(0)
+        load_q_scales(1)
+        nc.sync.dma_start(kw_pool[:, K_HEAD:T], k_flat[:, K_HEAD:T])
+        nc.sync.dma_start(qw[:], q_words[0, 0].rearrange("p n t -> p (n t)").bitcast(I32))
+        load_q_scales(2)
         for r in range(4):
             nc.sync.dma_start(
                 vb_pool[V_ROW + r : P : 32].bitcast(I32),
                 v_scales[:, r:16:4, :].rearrange("u f e -> f u e").bitcast(I32),
             )
+        load_q_scales(3)
+        nc.sync.dma_start(vw_pool[:], v_words.rearrange("u p e t -> p u (e t)").bitcast(I32))
 
         cols = PAGE // 16
         ks_g = held.tile([P, N], U8, name="ks_g", align_bytes=64)
@@ -103,8 +108,8 @@ def tile_attend_pkv8q_sigm_kernel(
                 kw_g[:, u].rearrange("p t m -> p m t"),
                 kw_pool[:].bitcast(U32).indirect(offs_t[:, u * cols : (u + 1) * cols]),
             )
-        vb_g = laid.tile([P, PAGES * DV], U8, name="vb_g", align_bytes=64, offset=0)
-        vw_g = laid.tile([P, PAGES * DV], U32, name="vw_g", align_bytes=64, offset=PAGES * DV)
+        vb_g = held.tile([P, PAGES * DV], U8, name="vb_g", align_bytes=64)
+        vw_g = held.tile([P, PAGES * DV], U32, name="vw_g", align_bytes=64)
 
         steps = [(b, u) for u in range(PAGES) for b in range(QB)]
         probs = {}
@@ -118,21 +123,32 @@ def tile_attend_pkv8q_sigm_kernel(
                     rhs=qw[:, qcols].bitcast(X4), rhs_scale=qs[:, qcols],
                     start=True, stop=True,
                 )
-            prob = ring.tile([P, P, 4], F32, name="prob", bufs=6)
-            nc.scalar.activation(prob[:], score[:].rearrange("p t q -> p q t"), ACT.Sigmoid)
+            if (b, u) == ON_SCALAR:
+                prob = held.tile([P, 4, P], F32, name="prob_tq")
+                nc.scalar.activation(prob[:], score[:], ACT.Sigmoid)
+            else:
+                prob = ring.tile([P, P, 4], F32, name="prob", bufs=5)
+                nc.scalar.activation(prob[:], score[:].rearrange("p t q -> p q t"), ACT.Sigmoid)
             probs[(b, u)] = prob
 
-        weights = {}
         packed = {}
         acc = [psum.tile([P, DV], F32, name="acc%d" % b) for b in range(QB)]
-        behind = {steps[3]: vw_at, steps[4]: vb_at}
+        weights = {}
 
         def weigh(b, u):
-            if (b, u) in behind:
-                w = laid.tile([P, P, 4], BF16, name="w%d%d" % (b, u), align_bytes=64, offset=behind[(b, u)])
+            if b == 1 and u > 0:
+                w = laid.tile([P, P, 4], BF16, name="w_late%d" % u, align_bytes=64, offset=2 * PAGE * u)
             else:
                 w = ring.tile([P, P, 4], BF16, name="w", bufs=4, align_bytes=64)
-            nc.vector.tensor_tensor(w[:], probs[(b, u)][:], vs_t[:, u, 0:4].unsqueeze(1).broadcast_to([P, P, 4]), MULT)
+            if (b, u) == ON_SCALAR:
+                w_tq = held.tile([P, 4, P], BF16, name="w_tq")
+                for t in range(4):
+                    nc.scalar.activation(w_tq[:, t, :], probs[(b, u)][:, t, :], ACT.Copy, scale=vs_t[:, u, t : t + 1])
+                nc.scalar.copy(w[:], w_tq[:].rearrange("p t q -> p q t"))
+            else:
+                nc.vector.tensor_tensor(
+                    w[:], probs[(b, u)][:], vs_t[:, u, 0:4].unsqueeze(1).broadcast_to([P, P, 4]), MULT
+                )
             weights[(b, u)] = w
 
         def quantise(b, u):
@@ -151,14 +167,13 @@ def tile_attend_pkv8q_sigm_kernel(
                 start=(u == 0), stop=(u == PAGES - 1),
             )
 
+        nc.vector.tensor_copy(vb_g[:], vb_pool[:].rearrange("p u e -> p (u e)").indirect(voffs_t[:]))
         weigh(*steps[0])
         for i in range(1, len(steps)):
             if i == 3:
                 nc.vector.tensor_copy(
                     vw_g[:], vw_pool[:].rearrange("p u e -> p (u e)").bitcast(U32).indirect(voffs_t[:])
                 )
-            if i == 4:
-                nc.vector.tensor_copy(vb_g[:], vb_pool[:].rearrange("p u e -> p (u e)").indirect(voffs_t[:]))
             weigh(*steps[i])
             quantise(*steps[i - 1])
         quantise(*steps[-1])

@@ -32,7 +32,6 @@ def tile_attend_pkv8q_sigm_kernel(
     nc = tc.nc
     with ExitStack() as ctx:
         held = ctx.enter_context(tc.tile_pool(name="held", bufs=1))
-        laid = ctx.enter_context(tc.tile_pool(name="laid", bufs=1))
         ring = ctx.enter_context(tc.tile_pool(name="ring", bufs=3))
         psum = ctx.enter_context(tc.psum_pool(name="psum", bufs=1))
 
@@ -46,7 +45,7 @@ def tile_attend_pkv8q_sigm_kernel(
         qw = held.tile([P, NQ], I32, name="qw", align_bytes=64)
         qs = held.tile([P, NQ], U8, name="qs", align_bytes=64)
         kw_pool = held.tile([P, T], I32, name="kw_pool", align_bytes=64)
-        vw_pool = laid.tile([P, POOL_PAGES, DV], I32, name="vw_pool", align_bytes=64, offset=0)
+        vw_pool = held.tile([P, POOL_PAGES, DV], I32, name="vw_pool", align_bytes=64)
         vb_pool = held.tile([P, POOL_PAGES, DV], U8, name="vb_pool", align_bytes=64)
 
         make_identity(nc, ident[:])
@@ -136,10 +135,7 @@ def tile_attend_pkv8q_sigm_kernel(
         weights = {}
 
         def weigh(b, u):
-            if b == 1 and u > 0:
-                w = laid.tile([P, P, 4], BF16, name="w_late%d" % u, align_bytes=64, offset=2 * PAGE * u)
-            else:
-                w = ring.tile([P, P, 4], BF16, name="w", bufs=4, align_bytes=64)
+            w = ring.tile([P, P, 4], BF16, name="w", bufs=6, align_bytes=64)
             if (b, u) == ON_SCALAR:
                 w_tq = held.tile([P, 4, P], BF16, name="w_tq")
                 for t in range(4):
@@ -167,19 +163,30 @@ def tile_attend_pkv8q_sigm_kernel(
                 start=(u == 0), stop=(u == PAGES - 1),
             )
 
+        def gather_values(lo, hi):
+            nc.vector.tensor_copy(
+                vw_g[:, lo * DV : hi * DV],
+                vw_pool[:].rearrange("p u e -> p (u e)").bitcast(U32).indirect(voffs_t[:, lo * vcols : hi * vcols]),
+            )
+
+        last = PAGES - 1
+        vcols = DV // 16
+        early = steps[: QB * last]
         nc.vector.tensor_copy(vb_g[:], vb_pool[:].rearrange("p u e -> p (u e)").indirect(voffs_t[:]))
-        weigh(*steps[0])
-        for i in range(1, len(steps)):
-            if i == 3:
-                nc.vector.tensor_copy(
-                    vw_g[:], vw_pool[:].rearrange("p u e -> p (u e)").bitcast(U32).indirect(voffs_t[:])
-                )
-            weigh(*steps[i])
-            quantise(*steps[i - 1])
-        quantise(*steps[-1])
-        for b, u in steps:
+        weigh(*early[0])
+        for before, step in zip(early, early[1:]):
+            weigh(*step)
+            quantise(*before)
+        gather_values(0, last)
+        quantise(*early[-1])
+        weigh(0, last)
+        weigh(1, last)
+        gather_values(last, PAGES)
+        quantise(1, last)
+        quantise(0, last)
+        for b, u in early + [(1, last), (0, last)]:
             multiply(b, u)
-        for b in range(QB):
+        for b in reversed(range(QB)):
             res = ring.tile([P, DV], F32, name="res", bufs=2)
             nc.scalar.activation(res[:], acc[b][:], ACT.Copy, scale=1.0 / 16.0)
             nc.sync.dma_start(out[0, b * P : (b + 1) * P, :], res[:])

@@ -51,21 +51,25 @@ def tile_attend_pkv8q_sigm_kernel(
         make_identity(nc, ident[:])
         nc.vector.memset(ks_pool[:].bitcast(I32), 0)
         nc.vector.memset(warm[:], 0.0)
+        nc.vector.memset(qs[:].bitcast(I32), 0)
         nc.vector.memset(vs_pool[0:VS_ROW, :], 0.0)
         nc.vector.memset(vb_pool[:].rearrange("p u e -> p (u e)").bitcast(I32), 0)
+        nc.scalar.dma_start(vs_pool[VS_ROW:P, :], vs[0:1, :])
         nc.scalar.activation(warm[:, 0:1], warm[:, 4:5], ACT.Sigmoid)
 
         k_flat = k_words[0].rearrange("p n t -> p (n t)").bitcast(I32)
 
-        def load_q_scales(quad):
-            rows = q_scales[0, 0, 4 * quad : 4 * quad + 4, :].bitcast(I32)
+        def load_q_scales(r):
+            nc.sync.dma_start(qs[r:P:32, :].bitcast(I32), q_scales[0, 0, r:16:4, :].bitcast(I32))
+
+        def load_v_scales(r):
             nc.sync.dma_start(
-                qs[32 * quad : 32 * quad + 32, :].bitcast(I32), rows.unsqueeze(0).broadcast_to([8, 4, NQ // 4])
+                vb_pool[V_ROW + r : P : 32].bitcast(I32),
+                v_scales[:, r:16:4, :].rearrange("u f e -> f u e").bitcast(I32),
             )
 
         nc.sync.dma_start(offs_t[:], offs)
         nc.sync.dma_start(voffs_t[:], voffs)
-        nc.sync.dma_start(vs_pool[VS_ROW:P, :], vs[0:1, :])
         nc.sync.dma_start(kw_pool[:, 0:K_HEAD], k_flat[:, 0:K_HEAD])
         for r in range(4):
             nc.sync.dma_start(ks_pool[r:P:32, :].bitcast(I32), k_scales[0, r:16:4, :].bitcast(I32))
@@ -75,10 +79,7 @@ def tile_attend_pkv8q_sigm_kernel(
         nc.sync.dma_start(qw[:], q_words[0, 0].rearrange("p n t -> p (n t)").bitcast(I32))
         load_q_scales(2)
         for r in range(4):
-            nc.sync.dma_start(
-                vb_pool[V_ROW + r : P : 32].bitcast(I32),
-                v_scales[:, r:16:4, :].rearrange("u f e -> f u e").bitcast(I32),
-            )
+            load_v_scales(r)
         load_q_scales(3)
         nc.sync.dma_start(vw_pool[:], v_words.rearrange("u p e t -> p u (e t)").bitcast(I32))
 

@@ -90,7 +90,8 @@ def tile_attend_pkv8q_sigm_kernel(
         kw_g = held.tile([P, PAGES, 4, P], U32, name="kw_g", align_bytes=64)
         vs_d = held.tile([P, PAGES, 4, P], F32, name="vs_d", align_bytes=64)
         vs_t = held.tile([P, PAGES, 8], F32, name="vs_t", align_bytes=64)
-        nc.vector.tensor_copy(vs_g[:].rearrange("p u j -> p (u j)"), vs_pool[:].indirect(offs_t[:]))
+        for u in range(PAGES):
+            nc.vector.tensor_copy(vs_g[:, u], vs_pool[:].indirect(offs_t[:, u * cols : (u + 1) * cols]))
         for u in range(PAGES):
             nc.scalar.copy(vs_d[:, u].rearrange("p t m -> p m t"), vs_g[:, u].rearrange("p (m t) -> p m t", t=4))
             turned = psum.tile([P, 4, P], F32, name="turned", bufs=2)
@@ -132,7 +133,9 @@ def tile_attend_pkv8q_sigm_kernel(
             probs[(b, u)] = prob
 
         packed = {}
-        acc = [psum.tile([P, DV], F32, name="acc%d" % b) for b in range(QB)]
+        spans = {0: [(0, DV // 2), (DV // 2, DV)], 1: [(0, DV)]}
+        acc = {(0, lo): psum.tile([P, hi - lo], F32, name="acc0_%d" % lo, tag="turned", bufs=2) for lo, hi in spans[0]}
+        acc[(1, 0)] = psum.tile([P, DV], F32, name="acc1")
         weights = {}
 
         def weigh(b, u):
@@ -156,13 +159,14 @@ def tile_attend_pkv8q_sigm_kernel(
 
         def multiply(b, u):
             codes, plane = packed[(b, u)]
-            ecols = slice(u * DV, (u + 1) * DV)
-            nc.tensor.matmul_mx(
-                acc[b][:],
-                lhsT=codes[:].bitcast(X4), lhsT_scale=plane[:],
-                rhs=vw_g[:, ecols].bitcast(X4), rhs_scale=vb_g[V_ROW:P, ecols],
-                start=(u == 0), stop=(u == PAGES - 1),
-            )
+            for lo, hi in spans[b]:
+                ecols = slice(u * DV + lo, u * DV + hi)
+                nc.tensor.matmul_mx(
+                    acc[(b, lo)][:],
+                    lhsT=codes[:].bitcast(X4), lhsT_scale=plane[:],
+                    rhs=vw_g[:, ecols].bitcast(X4), rhs_scale=vb_g[V_ROW:P, ecols],
+                    start=(u == 0), stop=(u == PAGES - 1),
+                )
 
         def gather_values(lo, hi):
             nc.vector.tensor_copy(
@@ -188,6 +192,10 @@ def tile_attend_pkv8q_sigm_kernel(
         for b, u in early + [(1, last), (0, last)]:
             multiply(b, u)
         for b in reversed(range(QB)):
-            res = ring.tile([P, DV], F32, name="res", bufs=2)
-            nc.scalar.activation(res[:], acc[b][:], ACT.Copy, scale=1.0 / 16.0)
-            nc.sync.dma_start(out[0, b * P : (b + 1) * P, :], res[:])
+            for lo, hi in spans[b]:
+                res = held.tile([P, hi - lo], F32, name="res%d_%d" % (b, lo))
+                if (b, lo) == (0, 0):
+                    nc.vector.tensor_scalar_mul(res[:], acc[(b, lo)][:], 1.0 / 16.0)
+                else:
+                    nc.scalar.activation(res[:], acc[(b, lo)][:], ACT.Copy, scale=1.0 / 16.0)
+                nc.sync.dma_start(out[0, b * P : (b + 1) * P, lo:hi], res[:])

@@ -1,7 +1,6 @@
 from contextlib import ExitStack
 
 import concourse.mybir as mybir
-from concourse.masks import make_identity
 
 N, T, D, DV, NQ, PAGE = 1536, 4096, 512, 256, 256, 512
 P = 128
@@ -22,7 +21,7 @@ MULT = mybir.AluOpType.mult
 
 V_ROW = 4
 VS_ROW = P - 1
-K_HEAD = T // 4
+K_HEAD = 7 * T // 32
 ON_SCALAR = (0, PAGES - 1)
 
 
@@ -40,7 +39,8 @@ def tile_attend_pkv8q_sigm_kernel(
         ks_pool = held.tile([P, T], U8, name="ks_pool", align_bytes=64)
         vs_pool = held.tile([P, T], F32, name="vs_pool", align_bytes=64)
         ident = held.tile([P, P], F32, name="ident", align_bytes=64)
-        warm = held.tile([P, 8], F32, name="warm")
+        zero = held.tile([P, 8], F32, name="zero", tag="skew", align_bytes=64)
+        half = held.tile([P, 8], F32, name="half")
 
         qw = held.tile([P, NQ], I32, name="qw", align_bytes=64)
         qs = held.tile([P, NQ], U8, name="qs", align_bytes=64)
@@ -48,14 +48,18 @@ def tile_attend_pkv8q_sigm_kernel(
         vw_pool = held.tile([P, POOL_PAGES, DV], I32, name="vw_pool", align_bytes=64)
         vb_pool = held.tile([P, POOL_PAGES, DV], U8, name="vb_pool", align_bytes=64)
 
-        make_identity(nc, ident[:])
         nc.vector.memset(ks_pool[:].bitcast(I32), 0)
-        nc.vector.memset(warm[:], 0.0)
+        nc.vector.memset(zero[:], 0.0)
         nc.vector.memset(qs[:].bitcast(I32), 0)
         nc.vector.memset(vs_pool[0:VS_ROW, :], 0.0)
         nc.vector.memset(vb_pool[:].rearrange("p u e -> p (u e)").bitcast(I32), 0)
         nc.scalar.dma_start(vs_pool[VS_ROW:P, :], vs[0:1, :])
-        nc.scalar.activation(warm[:, 0:1], warm[:, 4:5], ACT.Sigmoid)
+        nc.scalar.activation(half[:, 0:1], zero[:, 0:1], ACT.Sigmoid)
+        skew = held.tile([P, P], F32, name="skew", tag="skew", align_bytes=64)
+        nc.gpsimd.iota(skew[:], pattern=[[1, P]], base=0, channel_multiplier=-1, allow_small_or_imprecise_dtypes=True)
+        dist = held.tile([P, P], F32, name="dist", tag="vs_d", align_bytes=64)
+        nc.scalar.activation(dist[:], skew[:], ACT.Abs, scale=half[:, 0:1])
+        nc.scalar.activation(ident[:], dist[:], ACT.Relu, scale=-4.0, bias=1.0)
 
         k_flat = k_words[0].rearrange("p n t -> p (n t)").bitcast(I32)
 
@@ -88,7 +92,7 @@ def tile_attend_pkv8q_sigm_kernel(
         ks_t = held.tile([P, PAGES, 4, P], U8, name="ks_t", align_bytes=64)
         vs_g = held.tile([P, PAGES, PAGE], F32, name="vs_g", align_bytes=64)
         kw_g = held.tile([P, PAGES, 4, P], U32, name="kw_g", align_bytes=64)
-        vs_d = held.tile([P, PAGES, 4, P], F32, name="vs_d", align_bytes=64)
+        vs_d = held.tile([P, PAGES, 4, P], F32, name="vs_d", tag="vs_d", align_bytes=64)
         vs_t = held.tile([P, PAGES, 8], F32, name="vs_t", align_bytes=64)
         for u in range(PAGES):
             nc.vector.tensor_copy(vs_g[:, u], vs_pool[:].indirect(offs_t[:, u * cols : (u + 1) * cols]))

@@ -23,6 +23,7 @@ V_ROW = 4
 VS_ROW = P - 1
 K_HEAD = 7 * T // 32
 ON_SCALAR = (0, PAGES - 1)
+ON_GPSIMD = (0, 1)
 
 
 def tile_attend_pkv8q_sigm_kernel(
@@ -93,15 +94,17 @@ def tile_attend_pkv8q_sigm_kernel(
         vs_g = held.tile([P, PAGES, PAGE], F32, name="vs_g", align_bytes=64)
         kw_g = held.tile([P, PAGES, 4, P], U32, name="kw_g", align_bytes=64)
         vs_d = held.tile([P, PAGES, 4, P], F32, name="vs_d", tag="vs_d", align_bytes=64)
-        vs_t = held.tile([P, PAGES, 8], F32, name="vs_t", align_bytes=64)
+        vs_t = held.tile([P, PAGES, 4], F32, name="vs_t", align_bytes=64)
+        turned = psum.tile([P, 512], F32, name="turned")
         for u in range(PAGES):
             nc.vector.tensor_copy(vs_g[:, u], vs_pool[:].indirect(offs_t[:, u * cols : (u + 1) * cols]))
         for u in range(PAGES):
             nc.scalar.copy(vs_d[:, u].rearrange("p t m -> p m t"), vs_g[:, u].rearrange("p (m t) -> p m t", t=4))
-            turned = psum.tile([P, 4, P], F32, name="turned", bufs=2)
-            for t in range(4):
-                nc.tensor.transpose(turned[:, t, :], vs_d[:, u, t, :], ident[:])
-            nc.scalar.copy(vs_t[:, u, 0:4], turned[:, :, VS_ROW])
+            for t in reversed(range(4)):
+                first = 1 + 4 * (PAGES - 1 - u) + t
+                nc.tensor.transpose(turned[:, first : first + P], vs_d[:, u, t, :], ident[:])
+        vs_p = turned[:, P : P + 4 * PAGES].rearrange("p (u t) -> p u t", t=4)
+        nc.scalar.copy(vs_t[:], vs_p)
         for lo, hi in ((0, PAGES - 1), (PAGES - 1, PAGES)):
             nc.vector.tensor_copy(ks_g[:, lo * PAGE : hi * PAGE], ks_pool[:].indirect(offs_t[:, lo * cols : hi * cols]))
         for lo, hi in ((0, PAGES - 1), (PAGES - 1, PAGES)):
@@ -114,7 +117,6 @@ def tile_attend_pkv8q_sigm_kernel(
                 kw_pool[:].bitcast(U32).indirect(offs_t[:, u * cols : (u + 1) * cols]),
             )
         vb_g = held.tile([P, PAGES * DV], U8, name="vb_g", align_bytes=64)
-        vw_g = held.tile([P, PAGES * DV], U32, name="vw_g", align_bytes=64)
 
         steps = [(b, u) for u in range(PAGES) for b in range(QB)]
         probs = {}
@@ -131,6 +133,9 @@ def tile_attend_pkv8q_sigm_kernel(
             if (b, u) == ON_SCALAR:
                 prob = held.tile([P, 4, P], F32, name="prob_tq")
                 nc.scalar.activation(prob[:], score[:], ACT.Sigmoid)
+            elif (b, u) == ON_GPSIMD:
+                prob = held.tile([P, P, 4], F32, name="prob_pool", tag="vw_g", align_bytes=64)
+                nc.scalar.activation(prob[:], score[:].rearrange("p t q -> p q t"), ACT.Sigmoid)
             else:
                 prob = ring.tile([P, P, 4], F32, name="prob", bufs=5)
                 nc.scalar.activation(prob[:], score[:].rearrange("p t q -> p q t"), ACT.Sigmoid)
@@ -138,28 +143,37 @@ def tile_attend_pkv8q_sigm_kernel(
 
         packed = {}
         spans = {0: [(0, DV // 2), (DV // 2, DV)], 1: [(0, DV)]}
-        acc = {(0, lo): psum.tile([P, hi - lo], F32, name="acc0_%d" % lo, tag="turned", bufs=2) for lo, hi in spans[0]}
+        acc = {(0, lo): psum.tile([P, hi - lo], F32, name="acc0_%d" % lo) for lo, hi in spans[0]}
         acc[(1, 0)] = psum.tile([P, DV], F32, name="acc1")
-        weights = {}
+        early_w = [held.tile([P, PAGES - 1, P, 4], BF16, name="early_w%d" % b, align_bytes=64) for b in range(QB)]
+        last_w = [held.tile([P, 1, P, 4], BF16, name="last_w%d" % b, align_bytes=64) for b in range(QB)]
 
         def weigh(b, u):
-            w = ring.tile([P, P, 4], BF16, name="w", bufs=6, align_bytes=64)
+            w = early_w[b][:, u] if u < PAGES - 1 else last_w[b][:, 0]
             if (b, u) == ON_SCALAR:
                 w_tq = held.tile([P, 4, P], BF16, name="w_tq")
                 for t in range(4):
-                    nc.scalar.activation(w_tq[:, t, :], probs[(b, u)][:, t, :], ACT.Copy, scale=vs_t[:, u, t : t + 1])
-                nc.scalar.copy(w[:], w_tq[:].rearrange("p t q -> p q t"))
+                    nc.scalar.activation(w_tq[:, t, :], probs[(b, u)][:, t, :], ACT.Copy, scale=vs_t[:, PAGES - 1 - u, t : t + 1])
+                nc.scalar.copy(w, w_tq[:].rearrange("p t q -> p q t"))
+            elif (b, u) == ON_GPSIMD:
+                nc.gpsimd.tensor_tensor(
+                    w, probs[(b, u)][:], vs_t[:, PAGES - 1 - u, :].unsqueeze(1).broadcast_to([P, P, 4]), MULT
+                )
             else:
                 nc.vector.tensor_tensor(
-                    w[:], probs[(b, u)][:], vs_t[:, u, 0:4].unsqueeze(1).broadcast_to([P, P, 4]), MULT
+                    w, probs[(b, u)][:], vs_p[:, PAGES - 1 - u, :].unsqueeze(1).broadcast_to([P, P, 4]), MULT
                 )
-            weights[(b, u)] = w
 
-        def quantise(b, u):
-            codes = ring.tile([P, P], U32, name="codes", bufs=6, align_bytes=64)
-            plane = ring.tile([P, P], U8, name="plane", bufs=6, align_bytes=64)
-            nc.vector.quantize_mx(codes[:].bitcast(X4), plane[:], weights[(b, u)][:].rearrange("p q t -> p (q t)"))
-            packed[(b, u)] = (codes, plane)
+        def quantise(w, b, pages):
+            codes = held.tile([P, len(pages), P], U32, name="codes%d_%d" % (b, pages[0]), align_bytes=64)
+            plane = held.tile([P, len(pages), P], U8, name="plane%d_%d" % (b, pages[0]), align_bytes=64)
+            nc.vector.quantize_mx(
+                codes[:].rearrange("p u q -> p (u q)").bitcast(X4),
+                plane[:].rearrange("p u q -> p (u q)"),
+                w[:].rearrange("p u q t -> p (u q t)"),
+            )
+            for i, u in enumerate(pages):
+                packed[(b, u)] = (codes[:, i], plane[:, i])
 
         def multiply(b, u):
             codes, plane = packed[(b, u)]
@@ -167,7 +181,7 @@ def tile_attend_pkv8q_sigm_kernel(
                 ecols = slice(u * DV + lo, u * DV + hi)
                 nc.tensor.matmul_mx(
                     acc[(b, lo)][:],
-                    lhsT=codes[:].bitcast(X4), lhsT_scale=plane[:],
+                    lhsT=codes.bitcast(X4), lhsT_scale=plane,
                     rhs=vw_g[:, ecols].bitcast(X4), rhs_scale=vb_g[V_ROW:P, ecols],
                     start=(u == 0), stop=(u == PAGES - 1),
                 )
@@ -182,18 +196,18 @@ def tile_attend_pkv8q_sigm_kernel(
         vcols = DV // 16
         early = steps[: QB * last]
         nc.vector.tensor_copy(vb_g[:], vb_pool[:].rearrange("p u e -> p (u e)").indirect(voffs_t[:]))
-        weigh(*early[0])
-        for before, step in zip(early, early[1:]):
+        for step in early:
             weigh(*step)
-            quantise(*before)
+        vw_g = held.tile([P, PAGES * DV], U32, name="vw_g", tag="vw_g", align_bytes=64)
+        quantise(early_w[0], 0, list(range(last)))
         gather_values(0, last)
-        quantise(*early[-1])
+        quantise(early_w[1], 1, list(range(last)))
         weigh(0, last)
         weigh(1, last)
         gather_values(last, PAGES)
-        quantise(1, last)
-        quantise(0, last)
-        for b, u in early + [(1, last), (0, last)]:
+        quantise(last_w[1], 1, [last])
+        quantise(last_w[0], 0, [last])
+        for b, u in sorted(early) + [(1, last), (0, last)]:
             multiply(b, u)
         for b in reversed(range(QB)):
             for lo, hi in spans[b]:

@@ -23,7 +23,9 @@ V_ROW = 4
 VS_ROW = P - 1
 K_HEAD = 7 * T // 32
 ON_SCALAR = (0, PAGES - 1)
-ON_GPSIMD = (0, 1)
+ON_GPSIMD = (1, 0)
+SHARED = (0, 1)
+GPSIMD_Q = 32
 
 
 def tile_attend_pkv8q_sigm_kernel(
@@ -133,7 +135,7 @@ def tile_attend_pkv8q_sigm_kernel(
             if (b, u) == ON_SCALAR:
                 prob = held.tile([P, 4, P], F32, name="prob_tq")
                 nc.scalar.activation(prob[:], score[:], ACT.Sigmoid)
-            elif (b, u) == ON_GPSIMD:
+            elif (b, u) == SHARED:
                 prob = held.tile([P, P, 4], F32, name="prob_pool", tag="vw_g", align_bytes=64)
                 nc.scalar.activation(prob[:], score[:].rearrange("p t q -> p q t"), ACT.Sigmoid)
             else:
@@ -158,6 +160,15 @@ def tile_attend_pkv8q_sigm_kernel(
             elif (b, u) == ON_GPSIMD:
                 nc.gpsimd.tensor_tensor(
                     w, probs[(b, u)][:], vs_t[:, PAGES - 1 - u, :].unsqueeze(1).broadcast_to([P, P, 4]), MULT
+                )
+            elif (b, u) == SHARED:
+                nc.gpsimd.tensor_tensor(
+                    w[:, 0:GPSIMD_Q], probs[(b, u)][:, 0:GPSIMD_Q],
+                    vs_t[:, PAGES - 1 - u, :].unsqueeze(1).broadcast_to([P, GPSIMD_Q, 4]), MULT,
+                )
+                nc.vector.tensor_tensor(
+                    w[:, GPSIMD_Q:P], probs[(b, u)][:, GPSIMD_Q:P],
+                    vs_p[:, PAGES - 1 - u, :].unsqueeze(1).broadcast_to([P, P - GPSIMD_Q, 4]), MULT,
                 )
             else:
                 nc.vector.tensor_tensor(

@@ -49,19 +49,19 @@ def tile_attend_pkv8q_sigm_kernel(
         qs = held.tile([P, NQ], U8, name="qs", align_bytes=64)
         kw_pool = held.tile([P, T], I32, name="kw_pool", align_bytes=64)
         vw_pool = held.tile([P, POOL_PAGES, DV], I32, name="vw_pool", align_bytes=64)
-        vb_pool = held.tile([P, POOL_PAGES, DV], U8, name="vb_pool", align_bytes=64)
 
         nc.vector.memset(ks_pool[:].bitcast(I32), 0)
         nc.vector.memset(zero[:], 0.0)
         nc.vector.memset(qs[:].bitcast(I32), 0)
         nc.vector.memset(vs_pool[0:VS_ROW, :], 0.0)
-        nc.vector.memset(vb_pool[:].rearrange("p u e -> p (u e)").bitcast(I32), 0)
         nc.scalar.dma_start(vs_pool[VS_ROW:P, :], vs[0:1, :])
         nc.scalar.activation(half[:, 0:1], zero[:, 0:1], ACT.Sigmoid)
         skew = held.tile([P, P], F32, name="skew", tag="skew", align_bytes=64)
         nc.gpsimd.iota(skew[:], pattern=[[1, P]], base=0, channel_multiplier=-1, allow_small_or_imprecise_dtypes=True)
         dist = held.tile([P, P], F32, name="dist", tag="vs_d", align_bytes=64)
         nc.scalar.activation(dist[:], skew[:], ACT.Abs, scale=half[:, 0:1])
+        vb_pool = held.tile([P, POOL_PAGES, DV], U8, name="vb_pool", tag="skew", align_bytes=64)
+        nc.gpsimd.memset(vb_pool[:].rearrange("p u e -> p (u e)").bitcast(I32), 0)
         nc.scalar.activation(ident[:], dist[:], ACT.Relu, scale=-4.0, bias=1.0)
 
         k_flat = k_words[0].rearrange("p n t -> p (n t)").bitcast(I32)
@@ -156,7 +156,9 @@ def tile_attend_pkv8q_sigm_kernel(
                 w_tq = held.tile([P, 4, P], BF16, name="w_tq")
                 for t in range(4):
                     nc.scalar.activation(w_tq[:, t, :], probs[(b, u)][:, t, :], ACT.Copy, scale=vs_t[:, PAGES - 1 - u, t : t + 1])
-                nc.scalar.copy(w, w_tq[:].rearrange("p t q -> p q t"))
+                nc.scalar.copy(
+                    w.rearrange("p (c i) t -> p c t i", i=4), w_tq[:].rearrange("p t (c i) -> p c t i", i=4)
+                )
             elif (b, u) == ON_GPSIMD:
                 nc.gpsimd.tensor_tensor(
                     w, probs[(b, u)][:], vs_t[:, PAGES - 1 - u, :].unsqueeze(1).broadcast_to([P, P, 4]), MULT

@@ -26,6 +26,8 @@ ON_SCALAR = (0, PAGES - 1)
 ON_GPSIMD = (1, 0)
 SHARED = (0, 1)
 GPSIMD_Q = 32
+LAST = (1, PAGES - 1)
+EXTRA_Q = 48
 
 
 def tile_attend_pkv8q_sigm_kernel(
@@ -133,8 +135,12 @@ def tile_attend_pkv8q_sigm_kernel(
                     start=True, stop=True,
                 )
             if (b, u) == ON_SCALAR:
-                prob = held.tile([P, 4, P], F32, name="prob_tq")
-                nc.scalar.activation(prob[:], score[:], ACT.Sigmoid)
+                prob = held.tile([P, 4, P + EXTRA_Q], F32, name="prob_tq")
+                nc.scalar.activation(prob[:, :, 0:P], score[:], ACT.Sigmoid)
+            elif (b, u) == LAST:
+                prob = held.tile([P, P - EXTRA_Q, 4], F32, name="prob_last")
+                nc.scalar.activation(prob[:], score[:, :, EXTRA_Q:P].rearrange("p t q -> p q t"), ACT.Sigmoid)
+                nc.scalar.activation(probs[ON_SCALAR][:, :, P : P + EXTRA_Q], score[:, :, 0:EXTRA_Q], ACT.Sigmoid)
             elif (b, u) == SHARED:
                 prob = held.tile([P, P, 4], F32, name="prob_pool", tag="vw_g", align_bytes=64)
                 nc.scalar.activation(prob[:], score[:].rearrange("p t q -> p q t"), ACT.Sigmoid)
@@ -153,11 +159,15 @@ def tile_attend_pkv8q_sigm_kernel(
         def weigh(b, u):
             w = early_w[b][:, u] if u < PAGES - 1 else last_w[b][:, 0]
             if (b, u) == ON_SCALAR:
-                w_tq = held.tile([P, 4, P], BF16, name="w_tq")
+                w_tq = held.tile([P, 4, P + EXTRA_Q], BF16, name="w_tq")
                 for t in range(4):
                     nc.scalar.activation(w_tq[:, t, :], probs[(b, u)][:, t, :], ACT.Copy, scale=vs_t[:, PAGES - 1 - u, t : t + 1])
-                nc.scalar.copy(
-                    w.rearrange("p (c i) t -> p c t i", i=4), w_tq[:].rearrange("p t (c i) -> p c t i", i=4)
+                for dst, src in ((last_w[1][:, 0, 0:EXTRA_Q], w_tq[:, :, P : P + EXTRA_Q]), (w, w_tq[:, :, 0:P])):
+                    nc.scalar.copy(dst.rearrange("p (c i) t -> p c t i", i=4), src.rearrange("p t (c i) -> p c t i", i=4))
+            elif (b, u) == LAST:
+                nc.vector.tensor_tensor(
+                    w[:, EXTRA_Q:P], probs[(b, u)][:],
+                    vs_p[:, PAGES - 1 - u, :].unsqueeze(1).broadcast_to([P, P - EXTRA_Q, 4]), MULT,
                 )
             elif (b, u) == ON_GPSIMD:
                 nc.gpsimd.tensor_tensor(

@@ -21,7 +21,7 @@ MULT = mybir.AluOpType.mult
 
 V_ROW = 4
 VS_ROW = P - 1
-K_HEAD = 7 * T // 32
+K_HEAD = 5 * T // 32
 ON_SCALAR = (0, PAGES - 1)
 ON_GPSIMD = (1, 0)
 SHARED = (0, 1)
@@ -235,7 +235,7 @@ def tile_attend_pkv8q_sigm_kernel(
         for b in reversed(range(QB)):
             for lo, hi in spans[b]:
                 res = held.tile([P, hi - lo], F32, name="res%d_%d" % (b, lo))
-                if (b, lo) == (0, 0):
+                if lo == 0:
                     nc.vector.tensor_scalar_mul(res[:], acc[(b, lo)][:], 1.0 / 16.0)
                 else:
                     nc.scalar.activation(res[:], acc[(b, lo)][:], ACT.Copy, scale=1.0 / 16.0)

@@ -25,9 +25,9 @@ K_HEAD = 5 * T // 32
 ON_SCALAR = (0, PAGES - 1)
 ON_GPSIMD = (1, 0)
 SHARED = (0, 1)
-GPSIMD_Q = 32
+GPSIMD_Q = 16
 LAST = (1, PAGES - 1)
-EXTRA_Q = 48
+EXTRA_Q = 32
 
 
 def tile_attend_pkv8q_sigm_kernel(

@@ -19,9 +19,8 @@ X4 = mybir.dt.float8_e4m3fn_x4
 ACT = mybir.ActivationFunctionType
 MULT = mybir.AluOpType.mult
 
-V_ROW = 4
+SPREAD = P // 16
 VS_ROW = P - 1
-K_HEAD = 5 * T // 32
 ON_SCALAR = (0, PAGES - 1)
 ON_GPSIMD = (1, 0)
 SHARED = (0, 1)
@@ -50,58 +49,47 @@ def tile_attend_pkv8q_sigm_kernel(
         qw = held.tile([P, NQ], I32, name="qw", align_bytes=64)
         qs = held.tile([P, NQ], U8, name="qs", align_bytes=64)
         kw_pool = held.tile([P, T], I32, name="kw_pool", align_bytes=64)
-        vw_pool = held.tile([P, POOL_PAGES, DV], I32, name="vw_pool", align_bytes=64)
+        vb_pool = held.tile([P, POOL_PAGES, DV], U8, name="vb_pool", tag="kw_g", align_bytes=64)
+        vb_t = held.tile([P, PAGES * DV], U8, name="vb_t", align_bytes=64)
 
+        nc.vector.memset(qs[:].bitcast(I32), 0)
         nc.vector.memset(ks_pool[:].bitcast(I32), 0)
         nc.vector.memset(zero[:], 0.0)
-        nc.vector.memset(qs[:].bitcast(I32), 0)
+        nc.vector.memset(vb_pool[:].rearrange("p u e -> p (u e)").bitcast(I32), 0)
         nc.vector.memset(vs_pool[0:VS_ROW, :], 0.0)
         nc.scalar.dma_start(vs_pool[VS_ROW:P, :], vs[0:1, :])
+        nc.scalar.dma_start(ks_pool[0:P:SPREAD, :].bitcast(I32), k_scales[0].bitcast(I32))
         nc.scalar.activation(half[:, 0:1], zero[:, 0:1], ACT.Sigmoid)
+        nc.scalar.dma_start(
+            vb_pool[0:P:SPREAD].bitcast(I32), v_scales.rearrange("u f e -> f u e").bitcast(I32)
+        )
         skew = held.tile([P, P], F32, name="skew", tag="skew", align_bytes=64)
         nc.gpsimd.iota(skew[:], pattern=[[1, P]], base=0, channel_multiplier=-1, allow_small_or_imprecise_dtypes=True)
         dist = held.tile([P, P], F32, name="dist", tag="vs_d", align_bytes=64)
         nc.scalar.activation(dist[:], skew[:], ACT.Abs, scale=half[:, 0:1])
-        vb_pool = held.tile([P, POOL_PAGES, DV], U8, name="vb_pool", tag="skew", align_bytes=64)
-        nc.gpsimd.memset(vb_pool[:].rearrange("p u e -> p (u e)").bitcast(I32), 0)
         nc.scalar.activation(ident[:], dist[:], ACT.Relu, scale=-4.0, bias=1.0)
-
-        k_flat = k_words[0].rearrange("p n t -> p (n t)").bitcast(I32)
 
         def load_q_scales(r):
             nc.sync.dma_start(qs[r:P:32, :].bitcast(I32), q_scales[0, 0, r:16:4, :].bitcast(I32))
 
-        def load_v_scales(r):
-            nc.sync.dma_start(
-                vb_pool[V_ROW + r : P : 32].bitcast(I32),
-                v_scales[:, r:16:4, :].rearrange("u f e -> f u e").bitcast(I32),
-            )
-
         nc.sync.dma_start(offs_t[:], offs)
         nc.sync.dma_start(voffs_t[:], voffs)
-        nc.sync.dma_start(kw_pool[:, 0:K_HEAD], k_flat[:, 0:K_HEAD])
-        for r in range(4):
-            nc.sync.dma_start(ks_pool[r:P:32, :].bitcast(I32), k_scales[0, r:16:4, :].bitcast(I32))
-        load_q_scales(0)
-        load_q_scales(1)
-        nc.sync.dma_start(kw_pool[:, K_HEAD:T], k_flat[:, K_HEAD:T])
-        nc.sync.dma_start(qw[:], q_words[0, 0].rearrange("p n t -> p (n t)").bitcast(I32))
-        load_q_scales(2)
-        for r in range(4):
-            load_v_scales(r)
+        for r in range(3):
+            load_q_scales(r)
+        nc.sync.dma_start(kw_pool[:], k_words[0].rearrange("p n t -> p (n t)").bitcast(I32))
         load_q_scales(3)
-        nc.sync.dma_start(vw_pool[:], v_words.rearrange("u p e t -> p u (e t)").bitcast(I32))
+        nc.sync.dma_start(qw[:], q_words[0, 0].rearrange("p n t -> p (n t)").bitcast(I32))
 
         cols = PAGE // 16
-        ks_g = held.tile([P, N], U8, name="ks_g", align_bytes=64)
+        ks_g = held.tile([P, N], U8, name="ks_g", tag="ks_g", align_bytes=64)
         ks_t = held.tile([P, PAGES, 4, P], U8, name="ks_t", align_bytes=64)
         vs_g = held.tile([P, PAGES, PAGE], F32, name="vs_g", align_bytes=64)
-        kw_g = held.tile([P, PAGES, 4, P], U32, name="kw_g", align_bytes=64)
         vs_d = held.tile([P, PAGES, 4, P], F32, name="vs_d", tag="vs_d", align_bytes=64)
         vs_t = held.tile([P, PAGES, 4], F32, name="vs_t", align_bytes=64)
+        vb_g = held.tile([P, PAGES * DV], U8, name="vb_g", align_bytes=64)
         turned = psum.tile([P, 512], F32, name="turned")
         for u in range(PAGES):
-            nc.vector.tensor_copy(vs_g[:, u], vs_pool[:].indirect(offs_t[:, u * cols : (u + 1) * cols]))
+            nc.scalar.activation(vs_g[:, u], vs_pool[:].indirect(offs_t[:, u * cols : (u + 1) * cols]), ACT.Copy)
         for u in range(PAGES):
             nc.scalar.copy(vs_d[:, u].rearrange("p t m -> p m t"), vs_g[:, u].rearrange("p (m t) -> p m t", t=4))
             for t in reversed(range(4)):
@@ -115,12 +103,21 @@ def tile_attend_pkv8q_sigm_kernel(
             nc.vector.tensor_copy(
                 ks_t[:, lo:hi], ks_g[:, lo * PAGE : hi * PAGE].rearrange("p (u m t) -> p u t m", u=hi - lo, t=4)
             )
+        ks_rows = ks_t[:].rearrange("p u t m -> p (u t m)").bitcast(I32)
+        for r in range(1, 4):
+            nc.sync.dma_start(ks_rows[r:P:32], ks_rows[SPREAD * r : P : 32])
+        vw_pool = held.tile([P, POOL_PAGES, DV], I32, name="vw_pool", tag="ks_g", align_bytes=64)
+        nc.sync.dma_start(vw_pool[:], v_words.rearrange("u p e t -> p u (e t)").bitcast(I32))
+        nc.vector.tensor_copy(vb_g[:], vb_pool[:].rearrange("p u e -> p (u e)").indirect(voffs_t[:]))
+        nc.vector.memset(vb_t[:].bitcast(I32), 0)
+        for r in range(4):
+            nc.sync.dma_start(vb_t[:].bitcast(I32)[r:P:32], vb_g[:].bitcast(I32)[SPREAD * r : P : 32])
+        kw_g = held.tile([P, PAGES, 4, P], U32, name="kw_g", tag="kw_g", align_bytes=64)
         for u in range(PAGES):
             nc.vector.tensor_copy(
                 kw_g[:, u].rearrange("p t m -> p m t"),
                 kw_pool[:].bitcast(U32).indirect(offs_t[:, u * cols : (u + 1) * cols]),
             )
-        vb_g = held.tile([P, PAGES * DV], U8, name="vb_g", align_bytes=64)
 
         steps = [(b, u) for u in range(PAGES) for b in range(QB)]
         probs = {}
@@ -205,7 +202,7 @@ def tile_attend_pkv8q_sigm_kernel(
                 nc.tensor.matmul_mx(
                     acc[(b, lo)][:],
                     lhsT=codes.bitcast(X4), lhsT_scale=plane,
-                    rhs=vw_g[:, ecols].bitcast(X4), rhs_scale=vb_g[V_ROW:P, ecols],
+                    rhs=vw_g[:, ecols].bitcast(X4), rhs_scale=vb_t[:, ecols],
                     start=(u == 0), stop=(u == PAGES - 1),
                 )
 
@@ -218,7 +215,6 @@ def tile_attend_pkv8q_sigm_kernel(
         last = PAGES - 1
         vcols = DV // 16
         early = steps[: QB * last]
-        nc.vector.tensor_copy(vb_g[:], vb_pool[:].rearrange("p u e -> p (u e)").indirect(voffs_t[:]))
         for step in early:
             weigh(*step)
         vw_g = held.tile([P, PAGES * DV], U32, name="vw_g", tag="vw_g", align_bytes=64)

@@ -20,6 +20,7 @@ ACT = mybir.ActivationFunctionType
 MULT = mybir.AluOpType.mult
 
 SPREAD = P // 16
+K_HEAD = 6 * T // 32
 VS_ROW = P - 1
 ON_SCALAR = (0, PAGES - 1)
 ON_GPSIMD = (1, 0)
@@ -43,30 +44,27 @@ def tile_attend_pkv8q_sigm_kernel(
         ks_pool = held.tile([P, T], U8, name="ks_pool", align_bytes=64)
         vs_pool = held.tile([P, T], F32, name="vs_pool", align_bytes=64)
         ident = held.tile([P, P], F32, name="ident", align_bytes=64)
-        zero = held.tile([P, 8], F32, name="zero", tag="skew", align_bytes=64)
+        zero = held.tile([P, 8], F32, name="zero")
         half = held.tile([P, 8], F32, name="half")
 
         qw = held.tile([P, NQ], I32, name="qw", align_bytes=64)
         qs = held.tile([P, NQ], U8, name="qs", align_bytes=64)
-        kw_pool = held.tile([P, T], I32, name="kw_pool", align_bytes=64)
+        kw_pool = held.tile([P, T], I32, name="kw_pool", tag="kw_pool", align_bytes=64)
         vb_pool = held.tile([P, POOL_PAGES, DV], U8, name="vb_pool", tag="kw_g", align_bytes=64)
-        vb_t = held.tile([P, PAGES * DV], U8, name="vb_t", align_bytes=64)
 
         nc.vector.memset(qs[:].bitcast(I32), 0)
         nc.vector.memset(ks_pool[:].bitcast(I32), 0)
-        nc.vector.memset(zero[:], 0.0)
         nc.vector.memset(vb_pool[:].rearrange("p u e -> p (u e)").bitcast(I32), 0)
+        nc.vector.memset(zero[:], 0.0)
         nc.vector.memset(vs_pool[0:VS_ROW, :], 0.0)
         nc.scalar.dma_start(vs_pool[VS_ROW:P, :], vs[0:1, :])
-        nc.scalar.dma_start(ks_pool[0:P:SPREAD, :].bitcast(I32), k_scales[0].bitcast(I32))
         nc.scalar.activation(half[:, 0:1], zero[:, 0:1], ACT.Sigmoid)
-        nc.scalar.dma_start(
-            vb_pool[0:P:SPREAD].bitcast(I32), v_scales.rearrange("u f e -> f u e").bitcast(I32)
-        )
         skew = held.tile([P, P], F32, name="skew", tag="skew", align_bytes=64)
         nc.gpsimd.iota(skew[:], pattern=[[1, P]], base=0, channel_multiplier=-1, allow_small_or_imprecise_dtypes=True)
-        dist = held.tile([P, P], F32, name="dist", tag="vs_d", align_bytes=64)
+        dist = held.tile([P, P], F32, name="dist", tag="vs_g", align_bytes=64)
         nc.scalar.activation(dist[:], skew[:], ACT.Abs, scale=half[:, 0:1])
+        vb_t = held.tile([P, PAGES * DV], U8, name="vb_t", tag="skew", align_bytes=64)
+        nc.gpsimd.memset(vb_t[:].bitcast(I32), 0)
         nc.scalar.activation(ident[:], dist[:], ACT.Relu, scale=-4.0, bias=1.0)
 
         def load_q_scales(r):
@@ -74,29 +72,34 @@ def tile_attend_pkv8q_sigm_kernel(
 
         nc.sync.dma_start(offs_t[:], offs)
         nc.sync.dma_start(voffs_t[:], voffs)
-        for r in range(3):
+        k_flat = k_words[0].rearrange("p n t -> p (n t)").bitcast(I32)
+        nc.sync.dma_start(kw_pool[:, 0:K_HEAD], k_flat[:, 0:K_HEAD])
+        load_q_scales(0)
+        nc.sync.dma_start(ks_pool[0:P:SPREAD, :].bitcast(I32), k_scales[0].bitcast(I32))
+        nc.sync.dma_start(vb_pool[0:P:SPREAD].bitcast(I32), v_scales.rearrange("u f e -> f u e").bitcast(I32))
+        nc.sync.dma_start(kw_pool[:, K_HEAD:T], k_flat[:, K_HEAD:T])
+        for r in range(1, 4):
             load_q_scales(r)
-        nc.sync.dma_start(kw_pool[:], k_words[0].rearrange("p n t -> p (n t)").bitcast(I32))
-        load_q_scales(3)
         nc.sync.dma_start(qw[:], q_words[0, 0].rearrange("p n t -> p (n t)").bitcast(I32))
 
         cols = PAGE // 16
         ks_g = held.tile([P, N], U8, name="ks_g", tag="ks_g", align_bytes=64)
         ks_t = held.tile([P, PAGES, 4, P], U8, name="ks_t", align_bytes=64)
-        vs_g = held.tile([P, PAGES, PAGE], F32, name="vs_g", align_bytes=64)
-        vs_d = held.tile([P, PAGES, 4, P], F32, name="vs_d", tag="vs_d", align_bytes=64)
-        vs_t = held.tile([P, PAGES, 4], F32, name="vs_t", align_bytes=64)
+        vs_g = held.tile([P, PAGES, PAGE], F32, name="vs_g", tag="vs_g", align_bytes=64)
+        vs_d = held.tile([P, PAGES - 1, 4, P], F32, name="vs_d", align_bytes=64)
         vb_g = held.tile([P, PAGES * DV], U8, name="vb_g", align_bytes=64)
         turned = psum.tile([P, 512], F32, name="turned")
         for u in range(PAGES):
             nc.scalar.activation(vs_g[:, u], vs_pool[:].indirect(offs_t[:, u * cols : (u + 1) * cols]), ACT.Copy)
         for u in range(PAGES):
-            nc.scalar.copy(vs_d[:, u].rearrange("p t m -> p m t"), vs_g[:, u].rearrange("p (m t) -> p m t", t=4))
+            by_place = vs_g[:, u].rearrange("p (m t) -> p t m", t=4)
+            if u > 0:
+                nc.scalar.copy(vs_d[:, u - 1].rearrange("p t m -> p m t"), by_place.rearrange("p t m -> p m t"))
+                by_place = vs_d[:, u - 1]
             for t in reversed(range(4)):
                 first = 1 + 4 * (PAGES - 1 - u) + t
-                nc.tensor.transpose(turned[:, first : first + P], vs_d[:, u, t, :], ident[:])
+                nc.tensor.transpose(turned[:, first : first + P], by_place[:, t, :], ident[:])
         vs_p = turned[:, P : P + 4 * PAGES].rearrange("p (u t) -> p u t", t=4)
-        nc.scalar.copy(vs_t[:], vs_p)
         for lo, hi in ((0, PAGES - 1), (PAGES - 1, PAGES)):
             nc.vector.tensor_copy(ks_g[:, lo * PAGE : hi * PAGE], ks_pool[:].indirect(offs_t[:, lo * cols : hi * cols]))
         for lo, hi in ((0, PAGES - 1), (PAGES - 1, PAGES)):
@@ -109,7 +112,6 @@ def tile_attend_pkv8q_sigm_kernel(
         vw_pool = held.tile([P, POOL_PAGES, DV], I32, name="vw_pool", tag="ks_g", align_bytes=64)
         nc.sync.dma_start(vw_pool[:], v_words.rearrange("u p e t -> p u (e t)").bitcast(I32))
         nc.vector.tensor_copy(vb_g[:], vb_pool[:].rearrange("p u e -> p (u e)").indirect(voffs_t[:]))
-        nc.vector.memset(vb_t[:].bitcast(I32), 0)
         for r in range(4):
             nc.sync.dma_start(vb_t[:].bitcast(I32)[r:P:32], vb_g[:].bitcast(I32)[SPREAD * r : P : 32])
         kw_g = held.tile([P, PAGES, 4, P], U32, name="kw_g", tag="kw_g", align_bytes=64)
@@ -118,6 +120,9 @@ def tile_attend_pkv8q_sigm_kernel(
                 kw_g[:, u].rearrange("p t m -> p m t"),
                 kw_pool[:].bitcast(U32).indirect(offs_t[:, u * cols : (u + 1) * cols]),
             )
+
+        vs_t = held.tile([P, PAGES, 4], F32, name="vs_t", tag="kw_pool", align_bytes=64)
+        nc.vector.tensor_copy(vs_t[:], vs_p)
 
         steps = [(b, u) for u in range(PAGES) for b in range(QB)]
         probs = {}

@@ -20,7 +20,7 @@ ACT = mybir.ActivationFunctionType
 MULT = mybir.AluOpType.mult
 
 SPREAD = P // 16
-K_HEAD = 6 * T // 32
+K_HEAD = 5 * T // 32
 VS_ROW = P - 1
 ON_SCALAR = (0, PAGES - 1)
 ON_GPSIMD = (1, 0)
@@ -44,85 +44,80 @@ def tile_attend_pkv8q_sigm_kernel(
         ks_pool = held.tile([P, T], U8, name="ks_pool", align_bytes=64)
         vs_pool = held.tile([P, T], F32, name="vs_pool", align_bytes=64)
         ident = held.tile([P, P], F32, name="ident", align_bytes=64)
-        zero = held.tile([P, 8], F32, name="zero")
+        zero = held.tile([P, 8], F32, name="zero", tag="zero", align_bytes=64)
         half = held.tile([P, 8], F32, name="half")
 
         qw = held.tile([P, NQ], I32, name="qw", align_bytes=64)
         qs = held.tile([P, NQ], U8, name="qs", align_bytes=64)
-        kw_pool = held.tile([P, T], I32, name="kw_pool", tag="kw_pool", align_bytes=64)
-        vb_pool = held.tile([P, POOL_PAGES, DV], U8, name="vb_pool", tag="kw_g", align_bytes=64)
+        kw_pool = held.tile([P, T], I32, name="kw_pool", align_bytes=64)
 
-        nc.vector.memset(qs[:].bitcast(I32), 0)
         nc.vector.memset(ks_pool[:].bitcast(I32), 0)
-        nc.vector.memset(vb_pool[:].rearrange("p u e -> p (u e)").bitcast(I32), 0)
         nc.vector.memset(zero[:], 0.0)
         nc.vector.memset(vs_pool[0:VS_ROW, :], 0.0)
+        nc.vector.memset(qs[:].bitcast(I32), 0)
         nc.scalar.dma_start(vs_pool[VS_ROW:P, :], vs[0:1, :])
         nc.scalar.activation(half[:, 0:1], zero[:, 0:1], ACT.Sigmoid)
         skew = held.tile([P, P], F32, name="skew", tag="skew", align_bytes=64)
         nc.gpsimd.iota(skew[:], pattern=[[1, P]], base=0, channel_multiplier=-1, allow_small_or_imprecise_dtypes=True)
         dist = held.tile([P, P], F32, name="dist", tag="vs_g", align_bytes=64)
         nc.scalar.activation(dist[:], skew[:], ACT.Abs, scale=half[:, 0:1])
-        vb_t = held.tile([P, PAGES * DV], U8, name="vb_t", tag="skew", align_bytes=64)
-        nc.gpsimd.memset(vb_t[:].bitcast(I32), 0)
+        vb_pool = held.tile([P, POOL_PAGES, DV], U8, name="vb_pool", tag="skew", align_bytes=64)
+        nc.gpsimd.memset(vb_pool[:].rearrange("p u e -> p (u e)").bitcast(I32), 0)
         nc.scalar.activation(ident[:], dist[:], ACT.Relu, scale=-4.0, bias=1.0)
+        vb_t = held.tile([P, PAGES * DV], U8, name="vb_t", tag="zero", align_bytes=64)
+        nc.gpsimd.memset(vb_t[:].bitcast(I32), 0)
 
-        def load_q_scales(r):
-            nc.sync.dma_start(qs[r:P:32, :].bitcast(I32), q_scales[0, 0, r:16:4, :].bitcast(I32))
-
-        nc.sync.dma_start(offs_t[:], offs)
-        nc.sync.dma_start(voffs_t[:], voffs)
         k_flat = k_words[0].rearrange("p n t -> p (n t)").bitcast(I32)
         nc.sync.dma_start(kw_pool[:, 0:K_HEAD], k_flat[:, 0:K_HEAD])
-        load_q_scales(0)
-        nc.sync.dma_start(ks_pool[0:P:SPREAD, :].bitcast(I32), k_scales[0].bitcast(I32))
-        nc.sync.dma_start(vb_pool[0:P:SPREAD].bitcast(I32), v_scales.rearrange("u f e -> f u e").bitcast(I32))
+        nc.sync.dma_start(offs_t[:], offs)
+        for r in range(4):
+            nc.sync.dma_start(ks_pool[r:P:32, :].bitcast(I32), k_scales[0, r:16:4, :].bitcast(I32))
+        nc.sync.dma_start(voffs_t[:], voffs)
         nc.sync.dma_start(kw_pool[:, K_HEAD:T], k_flat[:, K_HEAD:T])
-        for r in range(1, 4):
-            load_q_scales(r)
         nc.sync.dma_start(qw[:], q_words[0, 0].rearrange("p n t -> p (n t)").bitcast(I32))
+        for r in range(4):
+            nc.sync.dma_start(qs[r:P:32, :].bitcast(I32), q_scales[0, 0, r:16:4, :].bitcast(I32))
+        nc.sync.dma_start(vb_pool[0:P:SPREAD].bitcast(I32), v_scales.rearrange("u f e -> f u e").bitcast(I32))
 
         cols = PAGE // 16
         ks_g = held.tile([P, N], U8, name="ks_g", tag="ks_g", align_bytes=64)
         ks_t = held.tile([P, PAGES, 4, P], U8, name="ks_t", align_bytes=64)
-        vs_g = held.tile([P, PAGES, PAGE], F32, name="vs_g", tag="vs_g", align_bytes=64)
-        vs_d = held.tile([P, PAGES - 1, 4, P], F32, name="vs_d", align_bytes=64)
+        vs_g = held.tile([P, PAGES - 1, PAGE], F32, name="vs_g", tag="vs_g", align_bytes=64)
+        vs_first = held.tile([P, 4, P], F32, name="vs_first", align_bytes=64)
+        vs_last = held.tile([P, 4, P], F32, name="vs_last", align_bytes=64)
+        kw_g = held.tile([P, PAGES, 4, P], U32, name="kw_g", align_bytes=64)
         vb_g = held.tile([P, PAGES * DV], U8, name="vb_g", align_bytes=64)
         turned = psum.tile([P, 512], F32, name="turned")
+        nc.vector.tensor_copy(
+            vs_first[:].bitcast(U32).rearrange("p t m -> p m t"), vs_pool[:].bitcast(U32).indirect(offs_t[:, 0:cols])
+        )
+        for u in range(1, PAGES):
+            nc.scalar.activation(vs_g[:, u - 1], vs_pool[:].indirect(offs_t[:, u * cols : (u + 1) * cols]), ACT.Copy)
+        nc.scalar.copy(vs_last[:].rearrange("p t m -> p m t"), vs_g[:, 1].rearrange("p (m t) -> p m t", t=4))
+        by_place = [vs_first[:], vs_g[:, 0].rearrange("p (m t) -> p t m", t=4), vs_last[:]]
         for u in range(PAGES):
-            nc.scalar.activation(vs_g[:, u], vs_pool[:].indirect(offs_t[:, u * cols : (u + 1) * cols]), ACT.Copy)
-        for u in range(PAGES):
-            by_place = vs_g[:, u].rearrange("p (m t) -> p t m", t=4)
-            if u > 0:
-                nc.scalar.copy(vs_d[:, u - 1].rearrange("p t m -> p m t"), by_place.rearrange("p t m -> p m t"))
-                by_place = vs_d[:, u - 1]
             for t in reversed(range(4)):
                 first = 1 + 4 * (PAGES - 1 - u) + t
-                nc.tensor.transpose(turned[:, first : first + P], by_place[:, t, :], ident[:])
+                nc.tensor.transpose(turned[:, first : first + P], by_place[u][:, t, :], ident[:])
         vs_p = turned[:, P : P + 4 * PAGES].rearrange("p (u t) -> p u t", t=4)
+        vs_t = held.tile([P, PAGES, 4], F32, name="vs_t", align_bytes=64)
+        nc.scalar.copy(vs_t[:], vs_p)
         for lo, hi in ((0, PAGES - 1), (PAGES - 1, PAGES)):
             nc.vector.tensor_copy(ks_g[:, lo * PAGE : hi * PAGE], ks_pool[:].indirect(offs_t[:, lo * cols : hi * cols]))
         for lo, hi in ((0, PAGES - 1), (PAGES - 1, PAGES)):
             nc.vector.tensor_copy(
                 ks_t[:, lo:hi], ks_g[:, lo * PAGE : hi * PAGE].rearrange("p (u m t) -> p u t m", u=hi - lo, t=4)
             )
-        ks_rows = ks_t[:].rearrange("p u t m -> p (u t m)").bitcast(I32)
-        for r in range(1, 4):
-            nc.sync.dma_start(ks_rows[r:P:32], ks_rows[SPREAD * r : P : 32])
         vw_pool = held.tile([P, POOL_PAGES, DV], I32, name="vw_pool", tag="ks_g", align_bytes=64)
         nc.sync.dma_start(vw_pool[:], v_words.rearrange("u p e t -> p u (e t)").bitcast(I32))
-        nc.vector.tensor_copy(vb_g[:], vb_pool[:].rearrange("p u e -> p (u e)").indirect(voffs_t[:]))
-        for r in range(4):
-            nc.sync.dma_start(vb_t[:].bitcast(I32)[r:P:32], vb_g[:].bitcast(I32)[SPREAD * r : P : 32])
-        kw_g = held.tile([P, PAGES, 4, P], U32, name="kw_g", tag="kw_g", align_bytes=64)
         for u in range(PAGES):
             nc.vector.tensor_copy(
                 kw_g[:, u].rearrange("p t m -> p m t"),
                 kw_pool[:].bitcast(U32).indirect(offs_t[:, u * cols : (u + 1) * cols]),
             )
-
-        vs_t = held.tile([P, PAGES, 4], F32, name="vs_t", tag="kw_pool", align_bytes=64)
-        nc.vector.tensor_copy(vs_t[:], vs_p)
+        nc.vector.tensor_copy(vb_g[:], vb_pool[:].rearrange("p u e -> p (u e)").indirect(voffs_t[:]))
+        for r in range(4):
+            nc.sync.dma_start(vb_t[:].bitcast(I32)[r:P:32], vb_g[:].bitcast(I32)[SPREAD * r : P : 32])
 
         steps = [(b, u) for u in range(PAGES) for b in range(QB)]
         probs = {}

@@ -20,7 +20,8 @@ ACT = mybir.ActivationFunctionType
 MULT = mybir.AluOpType.mult
 
 SPREAD = P // 16
-K_HEAD = 5 * T // 32
+K_HEAD = 4 * T // 32
+VS_FILL = (0, 775, 1552)
 VS_ROW = P - 1
 ON_SCALAR = (0, PAGES - 1)
 ON_GPSIMD = (1, 0)
@@ -42,74 +43,82 @@ def tile_attend_pkv8q_sigm_kernel(
         offs_t = held.tile([P, N // 16], U16, name="offs_t")
         voffs_t = held.tile([P, PAGES * DV // 16], U16, name="voffs_t")
         ks_pool = held.tile([P, T], U8, name="ks_pool", align_bytes=64)
-        vs_pool = held.tile([P, T], F32, name="vs_pool", align_bytes=64)
+        vs_pool = held.tile([P, T], F32, name="vs_pool", tag="vs_pool", align_bytes=64)
         ident = held.tile([P, P], F32, name="ident", align_bytes=64)
-        zero = held.tile([P, 8], F32, name="zero", tag="zero", align_bytes=64)
+        zero = held.tile([P, 8], F32, name="zero")
         half = held.tile([P, 8], F32, name="half")
 
         qw = held.tile([P, NQ], I32, name="qw", align_bytes=64)
         qs = held.tile([P, NQ], U8, name="qs", align_bytes=64)
         kw_pool = held.tile([P, T], I32, name="kw_pool", align_bytes=64)
 
-        nc.vector.memset(ks_pool[:].bitcast(I32), 0)
-        nc.vector.memset(zero[:], 0.0)
-        nc.vector.memset(vs_pool[0:VS_ROW, :], 0.0)
+        vb_pool = held.tile([P, POOL_PAGES, DV], U8, name="vb_pool", align_bytes=64)
+        skew = held.tile([P, P], F32, name="skew", align_bytes=64)
+
         nc.vector.memset(qs[:].bitcast(I32), 0)
+        nc.vector.memset(ks_pool[:].bitcast(I32), 0)
+        nc.vector.memset(zero[:, 0:1], 0.0)
+        for lo, hi in zip(VS_FILL, VS_FILL[1:]):
+            nc.vector.memset(vs_pool[0:VS_ROW, lo:hi], 0.0)
+        nc.gpsimd.iota(skew[:], pattern=[[1, P]], base=0, channel_multiplier=-1, allow_small_or_imprecise_dtypes=True)
+        nc.gpsimd.memset(vs_pool[0:VS_ROW, VS_FILL[-1] : T], 0.0)
+        nc.gpsimd.memset(vb_pool[:].rearrange("p u e -> p (u e)").bitcast(I32), 0)
         nc.scalar.dma_start(vs_pool[VS_ROW:P, :], vs[0:1, :])
         nc.scalar.activation(half[:, 0:1], zero[:, 0:1], ACT.Sigmoid)
-        skew = held.tile([P, P], F32, name="skew", tag="skew", align_bytes=64)
-        nc.gpsimd.iota(skew[:], pattern=[[1, P]], base=0, channel_multiplier=-1, allow_small_or_imprecise_dtypes=True)
         dist = held.tile([P, P], F32, name="dist", tag="vs_g", align_bytes=64)
         nc.scalar.activation(dist[:], skew[:], ACT.Abs, scale=half[:, 0:1])
-        vb_pool = held.tile([P, POOL_PAGES, DV], U8, name="vb_pool", tag="skew", align_bytes=64)
-        nc.gpsimd.memset(vb_pool[:].rearrange("p u e -> p (u e)").bitcast(I32), 0)
         nc.scalar.activation(ident[:], dist[:], ACT.Relu, scale=-4.0, bias=1.0)
-        vb_t = held.tile([P, PAGES * DV], U8, name="vb_t", tag="zero", align_bytes=64)
-        nc.gpsimd.memset(vb_t[:].bitcast(I32), 0)
+
+        def load_q_scales(r):
+            nc.sync.dma_start(qs[r:P:32, :].bitcast(I32), q_scales[0, 0, r:16:4, :].bitcast(I32))
 
         k_flat = k_words[0].rearrange("p n t -> p (n t)").bitcast(I32)
-        nc.sync.dma_start(kw_pool[:, 0:K_HEAD], k_flat[:, 0:K_HEAD])
         nc.sync.dma_start(offs_t[:], offs)
-        for r in range(4):
-            nc.sync.dma_start(ks_pool[r:P:32, :].bitcast(I32), k_scales[0, r:16:4, :].bitcast(I32))
+        nc.sync.dma_start(kw_pool[:, 0:K_HEAD], k_flat[:, 0:K_HEAD])
         nc.sync.dma_start(voffs_t[:], voffs)
-        nc.sync.dma_start(kw_pool[:, K_HEAD:T], k_flat[:, K_HEAD:T])
+        nc.sync.dma_start(ks_pool[0:P:SPREAD, :].bitcast(I32), k_scales[0].bitcast(I32))
         nc.sync.dma_start(qw[:], q_words[0, 0].rearrange("p n t -> p (n t)").bitcast(I32))
-        for r in range(4):
-            nc.sync.dma_start(qs[r:P:32, :].bitcast(I32), q_scales[0, 0, r:16:4, :].bitcast(I32))
+        load_q_scales(0)
+        nc.sync.dma_start(kw_pool[:, K_HEAD:T], k_flat[:, K_HEAD:T])
+        for r in range(1, 4):
+            load_q_scales(r)
         nc.sync.dma_start(vb_pool[0:P:SPREAD].bitcast(I32), v_scales.rearrange("u f e -> f u e").bitcast(I32))
 
         cols = PAGE // 16
         ks_g = held.tile([P, N], U8, name="ks_g", tag="ks_g", align_bytes=64)
         ks_t = held.tile([P, PAGES, 4, P], U8, name="ks_t", align_bytes=64)
-        vs_g = held.tile([P, PAGES - 1, PAGE], F32, name="vs_g", tag="vs_g", align_bytes=64)
-        vs_first = held.tile([P, 4, P], F32, name="vs_first", align_bytes=64)
-        vs_last = held.tile([P, 4, P], F32, name="vs_last", align_bytes=64)
-        kw_g = held.tile([P, PAGES, 4, P], U32, name="kw_g", align_bytes=64)
+        vs_g = held.tile([P, PAGE], F32, name="vs_g", tag="vs_g", align_bytes=64)
+        vs_d = [held.tile([P, 4, P], F32, name="vs_d%d" % u, align_bytes=64) for u in range(PAGES)]
         vb_g = held.tile([P, PAGES * DV], U8, name="vb_g", align_bytes=64)
         turned = psum.tile([P, 512], F32, name="turned")
-        nc.vector.tensor_copy(
-            vs_first[:].bitcast(U32).rearrange("p t m -> p m t"), vs_pool[:].bitcast(U32).indirect(offs_t[:, 0:cols])
-        )
-        for u in range(1, PAGES):
-            nc.scalar.activation(vs_g[:, u - 1], vs_pool[:].indirect(offs_t[:, u * cols : (u + 1) * cols]), ACT.Copy)
-        nc.scalar.copy(vs_last[:].rearrange("p t m -> p m t"), vs_g[:, 1].rearrange("p (m t) -> p m t", t=4))
-        by_place = [vs_first[:], vs_g[:, 0].rearrange("p (m t) -> p t m", t=4), vs_last[:]]
-        for u in range(PAGES):
-            for t in reversed(range(4)):
-                first = 1 + 4 * (PAGES - 1 - u) + t
-                nc.tensor.transpose(turned[:, first : first + P], by_place[u][:, t, :], ident[:])
-        vs_p = turned[:, P : P + 4 * PAGES].rearrange("p (u t) -> p u t", t=4)
-        vs_t = held.tile([P, PAGES, 4], F32, name="vs_t", align_bytes=64)
-        nc.scalar.copy(vs_t[:], vs_p)
         for lo, hi in ((0, PAGES - 1), (PAGES - 1, PAGES)):
             nc.vector.tensor_copy(ks_g[:, lo * PAGE : hi * PAGE], ks_pool[:].indirect(offs_t[:, lo * cols : hi * cols]))
         for lo, hi in ((0, PAGES - 1), (PAGES - 1, PAGES)):
             nc.vector.tensor_copy(
                 ks_t[:, lo:hi], ks_g[:, lo * PAGE : hi * PAGE].rearrange("p (u m t) -> p u t m", u=hi - lo, t=4)
             )
+        ks_rows = ks_t[:].rearrange("p u t m -> p (u t m)").bitcast(I32)
+        for r in range(1, 4):
+            nc.sync.dma_start(ks_rows[r:P:32], ks_rows[SPREAD * r : P : 32])
+        nc.scalar.activation(vs_g[:], vs_pool[:].indirect(offs_t[:, 0:cols]), ACT.Copy)
+        nc.scalar.copy(vs_d[0][:].rearrange("p t m -> p m t"), vs_g[:].rearrange("p (m t) -> p m t", t=4))
+        for u in range(1, PAGES):
+            nc.vector.tensor_copy(
+                vs_d[u][:].bitcast(U32).rearrange("p t m -> p m t"),
+                vs_pool[:].bitcast(U32).indirect(offs_t[:, u * cols : (u + 1) * cols]),
+            )
+        for u in range(PAGES):
+            for t in reversed(range(4)):
+                first = 1 + 4 * (PAGES - 1 - u) + t
+                nc.tensor.transpose(turned[:, first : first + P], vs_d[u][:, t, :], ident[:])
+        vs_p = turned[:, P : P + 4 * PAGES].rearrange("p (u t) -> p u t", t=4)
+        vs_t = held.tile([P, PAGES, 4], F32, name="vs_t", align_bytes=64)
+        nc.scalar.copy(vs_t[:], vs_p)
+        vb_t = held.tile([P, PAGES * DV], U8, name="vb_t", tag="vs_g", align_bytes=64)
+        nc.gpsimd.memset(vb_t[:].bitcast(I32), 0)
         vw_pool = held.tile([P, POOL_PAGES, DV], I32, name="vw_pool", tag="ks_g", align_bytes=64)
         nc.sync.dma_start(vw_pool[:], v_words.rearrange("u p e t -> p u (e t)").bitcast(I32))
+        kw_g = held.tile([P, PAGES, 4, P], U32, name="kw_g", tag="vs_pool", align_bytes=64)
         for u in range(PAGES):
             nc.vector.tensor_copy(
                 kw_g[:, u].rearrange("p t m -> p m t"),

@@ -22,13 +22,12 @@ MULT = mybir.AluOpType.mult
 SPREAD = P // 16
 K_HEAD = 4 * T // 32
 VS_FILL = (0, 775, 1552)
+QS_FILL = 33
 VS_ROW = P - 1
 ON_SCALAR = (0, PAGES - 1)
 ON_GPSIMD = (1, 0)
 SHARED = (0, 1)
 GPSIMD_Q = 16
-LAST = (1, PAGES - 1)
-EXTRA_Q = 32
 
 
 def tile_attend_pkv8q_sigm_kernel(
@@ -55,8 +54,9 @@ def tile_attend_pkv8q_sigm_kernel(
         vb_pool = held.tile([P, POOL_PAGES, DV], U8, name="vb_pool", align_bytes=64)
         skew = held.tile([P, P], F32, name="skew", align_bytes=64)
 
-        nc.vector.memset(qs[:].bitcast(I32), 0)
         nc.vector.memset(ks_pool[:].bitcast(I32), 0)
+        for lo, hi in ((0, QS_FILL), (QS_FILL, NQ // 4)):
+            nc.vector.memset(qs[:].bitcast(I32)[:, lo:hi], 0)
         nc.vector.memset(zero[:, 0:1], 0.0)
         for lo, hi in zip(VS_FILL, VS_FILL[1:]):
             nc.vector.memset(vs_pool[0:VS_ROW, lo:hi], 0.0)
@@ -77,10 +77,11 @@ def tile_attend_pkv8q_sigm_kernel(
         nc.sync.dma_start(kw_pool[:, 0:K_HEAD], k_flat[:, 0:K_HEAD])
         nc.sync.dma_start(voffs_t[:], voffs)
         nc.sync.dma_start(ks_pool[0:P:SPREAD, :].bitcast(I32), k_scales[0].bitcast(I32))
-        nc.sync.dma_start(qw[:], q_words[0, 0].rearrange("p n t -> p (n t)").bitcast(I32))
-        load_q_scales(0)
+        for r in range(2):
+            load_q_scales(r)
         nc.sync.dma_start(kw_pool[:, K_HEAD:T], k_flat[:, K_HEAD:T])
-        for r in range(1, 4):
+        nc.sync.dma_start(qw[:], q_words[0, 0].rearrange("p n t -> p (n t)").bitcast(I32))
+        for r in range(2, 4):
             load_q_scales(r)
         nc.sync.dma_start(vb_pool[0:P:SPREAD].bitcast(I32), v_scales.rearrange("u f e -> f u e").bitcast(I32))
 
@@ -141,12 +142,8 @@ def tile_attend_pkv8q_sigm_kernel(
                     start=True, stop=True,
                 )
             if (b, u) == ON_SCALAR:
-                prob = held.tile([P, 4, P + EXTRA_Q], F32, name="prob_tq")
-                nc.scalar.activation(prob[:, :, 0:P], score[:], ACT.Sigmoid)
-            elif (b, u) == LAST:
-                prob = held.tile([P, P - EXTRA_Q, 4], F32, name="prob_last")
-                nc.scalar.activation(prob[:], score[:, :, EXTRA_Q:P].rearrange("p t q -> p q t"), ACT.Sigmoid)
-                nc.scalar.activation(probs[ON_SCALAR][:, :, P : P + EXTRA_Q], score[:, :, 0:EXTRA_Q], ACT.Sigmoid)
+                prob = held.tile([P, 4, P], F32, name="prob_tq")
+                nc.scalar.activation(prob[:], score[:], ACT.Sigmoid)
             elif (b, u) == SHARED:
                 prob = held.tile([P, P, 4], F32, name="prob_pool", tag="vw_g", align_bytes=64)
                 nc.scalar.activation(prob[:], score[:].rearrange("p t q -> p q t"), ACT.Sigmoid)
@@ -165,16 +162,10 @@ def tile_attend_pkv8q_sigm_kernel(
         def weigh(b, u):
             w = early_w[b][:, u] if u < PAGES - 1 else last_w[b][:, 0]
             if (b, u) == ON_SCALAR:
-                w_tq = held.tile([P, 4, P + EXTRA_Q], BF16, name="w_tq")
+                w_tq = held.tile([P, 4, P], BF16, name="w_tq")
                 for t in range(4):
                     nc.scalar.activation(w_tq[:, t, :], probs[(b, u)][:, t, :], ACT.Copy, scale=vs_t[:, PAGES - 1 - u, t : t + 1])
-                for dst, src in ((last_w[1][:, 0, 0:EXTRA_Q], w_tq[:, :, P : P + EXTRA_Q]), (w, w_tq[:, :, 0:P])):
-                    nc.scalar.copy(dst.rearrange("p (c i) t -> p c t i", i=4), src.rearrange("p t (c i) -> p c t i", i=4))
-            elif (b, u) == LAST:
-                nc.vector.tensor_tensor(
-                    w[:, EXTRA_Q:P], probs[(b, u)][:],
-                    vs_p[:, PAGES - 1 - u, :].unsqueeze(1).broadcast_to([P, P - EXTRA_Q, 4]), MULT,
-                )
+                nc.scalar.copy(w.rearrange("p (c i) t -> p c t i", i=4), w_tq[:].rearrange("p t (c i) -> p c t i", i=4))
             elif (b, u) == ON_GPSIMD:
                 nc.gpsimd.tensor_tensor(
                     w, probs[(b, u)][:], vs_t[:, PAGES - 1 - u, :].unsqueeze(1).broadcast_to([P, P, 4]), MULT

@@ -23,6 +23,7 @@ SPREAD = P // 16
 K_HEAD = 4 * T // 32
 VS_FILL = (0, 775, 1552)
 QS_FILL = 33
+V_ROW = 4
 VS_ROW = P - 1
 ON_SCALAR = (0, PAGES - 1)
 ON_GPSIMD = (1, 0)
@@ -115,8 +116,6 @@ def tile_attend_pkv8q_sigm_kernel(
         vs_p = turned[:, P : P + 4 * PAGES].rearrange("p (u t) -> p u t", t=4)
         vs_t = held.tile([P, PAGES, 4], F32, name="vs_t", align_bytes=64)
         nc.scalar.copy(vs_t[:], vs_p)
-        vb_t = held.tile([P, PAGES * DV], U8, name="vb_t", tag="vs_g", align_bytes=64)
-        nc.gpsimd.memset(vb_t[:].bitcast(I32), 0)
         vw_pool = held.tile([P, POOL_PAGES, DV], I32, name="vw_pool", tag="ks_g", align_bytes=64)
         nc.sync.dma_start(vw_pool[:], v_words.rearrange("u p e t -> p u (e t)").bitcast(I32))
         kw_g = held.tile([P, PAGES, 4, P], U32, name="kw_g", tag="vs_pool", align_bytes=64)
@@ -126,8 +125,6 @@ def tile_attend_pkv8q_sigm_kernel(
                 kw_pool[:].bitcast(U32).indirect(offs_t[:, u * cols : (u + 1) * cols]),
             )
         nc.vector.tensor_copy(vb_g[:], vb_pool[:].rearrange("p u e -> p (u e)").indirect(voffs_t[:]))
-        for r in range(4):
-            nc.sync.dma_start(vb_t[:].bitcast(I32)[r:P:32], vb_g[:].bitcast(I32)[SPREAD * r : P : 32])
 
         steps = [(b, u) for u in range(PAGES) for b in range(QB)]
         probs = {}
@@ -151,6 +148,9 @@ def tile_attend_pkv8q_sigm_kernel(
                 prob = ring.tile([P, P, 4], F32, name="prob", bufs=5)
                 nc.scalar.activation(prob[:], score[:].rearrange("p t q -> p q t"), ACT.Sigmoid)
             probs[(b, u)] = prob
+
+        for r in range(4):
+            nc.sync.dma_start(ks_rows[V_ROW + r : P : 32, 0 : PAGES * DV // 4], vb_g[:].bitcast(I32)[SPREAD * r : P : 32])
 
         packed = {}
         spans = {0: [(0, DV // 2), (DV // 2, DV)], 1: [(0, DV)]}
@@ -202,7 +202,7 @@ def tile_attend_pkv8q_sigm_kernel(
                 nc.tensor.matmul_mx(
                     acc[(b, lo)][:],
                     lhsT=codes.bitcast(X4), lhsT_scale=plane,
-                    rhs=vw_g[:, ecols].bitcast(X4), rhs_scale=vb_t[:, ecols],
+                    rhs=vw_g[:, ecols].bitcast(X4), rhs_scale=ks_t[:].rearrange("p u t m -> p (u t m)")[V_ROW:P, ecols],
                     start=(u == 0), stop=(u == PAGES - 1),
                 )
 

@@ -43,7 +43,7 @@ def tile_attend_pkv8q_sigm_kernel(
         offs_t = held.tile([P, N // 16], U16, name="offs_t")
         voffs_t = held.tile([P, PAGES * DV // 16], U16, name="voffs_t")
         ks_pool = held.tile([P, T], U8, name="ks_pool", align_bytes=64)
-        vs_pool = held.tile([P, T], F32, name="vs_pool", tag="vs_pool", align_bytes=64)
+        vs_pool = held.tile([P, T], F32, name="vs_pool", align_bytes=64)
         ident = held.tile([P, P], F32, name="ident", align_bytes=64)
         zero = held.tile([P, 8], F32, name="zero")
         half = held.tile([P, 8], F32, name="half")
@@ -89,8 +89,7 @@ def tile_attend_pkv8q_sigm_kernel(
         cols = PAGE // 16
         ks_g = held.tile([P, N], U8, name="ks_g", tag="ks_g", align_bytes=64)
         ks_t = held.tile([P, PAGES, 4, P], U8, name="ks_t", align_bytes=64)
-        vs_g = held.tile([P, PAGE], F32, name="vs_g", tag="vs_g", align_bytes=64)
-        vs_d = [held.tile([P, 4, P], F32, name="vs_d%d" % u, align_bytes=64) for u in range(PAGES)]
+        vs_d = [held.tile([P, 4, P], F32, name="vs_d%d" % u, tag="vs_d%d" % u, align_bytes=64) for u in range(PAGES)]
         vb_g = held.tile([P, PAGES * DV], U8, name="vb_g", align_bytes=64)
         turned = psum.tile([P, 512], F32, name="turned")
         for lo, hi in ((0, PAGES - 1), (PAGES - 1, PAGES)):
@@ -102,23 +101,31 @@ def tile_attend_pkv8q_sigm_kernel(
         ks_rows = ks_t[:].rearrange("p u t m -> p (u t m)").bitcast(I32)
         for r in range(1, 4):
             nc.sync.dma_start(ks_rows[r:P:32], ks_rows[SPREAD * r : P : 32])
-        nc.scalar.activation(vs_g[:], vs_pool[:].indirect(offs_t[:, 0:cols]), ACT.Copy)
-        nc.scalar.copy(vs_d[0][:].rearrange("p t m -> p m t"), vs_g[:].rearrange("p (m t) -> p m t", t=4))
-        for u in range(1, PAGES):
-            nc.vector.tensor_copy(
-                vs_d[u][:].bitcast(U32).rearrange("p t m -> p m t"),
-                vs_pool[:].bitcast(U32).indirect(offs_t[:, u * cols : (u + 1) * cols]),
-            )
-        for u in range(PAGES):
-            for t in reversed(range(4)):
-                first = 1 + 4 * (PAGES - 1 - u) + t
-                nc.tensor.transpose(turned[:, first : first + P], vs_d[u][:, t, :], ident[:])
-        vs_p = turned[:, P : P + 4 * PAGES].rearrange("p (u t) -> p u t", t=4)
+        last = PAGES - 1
+        for u in (0, last):
+            vs_g = held.tile([P, PAGE], F32, name="vs_g%d" % u, tag="vs_g", align_bytes=64)
+            nc.scalar.activation(vs_g[:], vs_pool[:].indirect(offs_t[:, u * cols : (u + 1) * cols]), ACT.Copy)
+            nc.scalar.copy(vs_d[u][:].rearrange("p t m -> p m t"), vs_g[:].rearrange("p (m t) -> p m t", t=4))
+        nc.vector.tensor_copy(
+            vs_d[1][:].bitcast(U32).rearrange("p t m -> p m t"),
+            vs_pool[:].bitcast(U32).indirect(offs_t[:, cols : 2 * cols]),
+        )
         vs_t = held.tile([P, PAGES, 4], F32, name="vs_t", align_bytes=64)
-        nc.scalar.copy(vs_t[:], vs_p)
+        vs_p = {}
+
+        def turn(bank, pages):
+            for i, u in enumerate(pages):
+                base = 1 + 4 * (len(pages) - 1 - i)
+                for t in reversed(range(4)):
+                    nc.tensor.transpose(bank[:, base + t : base + t + P], vs_d[u][:, t, :], ident[:])
+                vs_p[u] = bank[:, base + VS_ROW : base + VS_ROW + 4]
+            for u in pages:
+                nc.scalar.copy(vs_t[:, u], vs_p[u])
+
+        turn(turned, range(last))
         vw_pool = held.tile([P, POOL_PAGES, DV], I32, name="vw_pool", tag="ks_g", align_bytes=64)
         nc.sync.dma_start(vw_pool[:], v_words.rearrange("u p e t -> p u (e t)").bitcast(I32))
-        kw_g = held.tile([P, PAGES, 4, P], U32, name="kw_g", tag="vs_pool", align_bytes=64)
+        kw_g = held.tile([P, PAGES, 4, P], U32, name="kw_g", tag="vs_d0", align_bytes=64)
         for u in range(PAGES):
             nc.vector.tensor_copy(
                 kw_g[:, u].rearrange("p t m -> p m t"),
@@ -129,7 +136,7 @@ def tile_attend_pkv8q_sigm_kernel(
         steps = [(b, u) for u in range(PAGES) for b in range(QB)]
         probs = {}
         for b, u in steps:
-            score = psum.tile([P, 4, P], F32, name="score", bufs=4)
+            score = psum.tile([P, 4, P], F32, name="score", tag="score", bufs=4)
             qcols = slice(b * P, (b + 1) * P)
             for t in range(4):
                 nc.tensor.matmul_mx(
@@ -149,6 +156,8 @@ def tile_attend_pkv8q_sigm_kernel(
                 nc.scalar.activation(prob[:], score[:].rearrange("p t q -> p q t"), ACT.Sigmoid)
             probs[(b, u)] = prob
 
+        turned_last = psum.tile([P, 512], F32, name="turned_last", tag="score", bufs=4)
+        turn(turned_last, [last])
         for r in range(4):
             nc.sync.dma_start(ks_rows[V_ROW + r : P : 32, 0 : PAGES * DV // 4], vb_g[:].bitcast(I32)[SPREAD * r : P : 32])
 
@@ -164,24 +173,24 @@ def tile_attend_pkv8q_sigm_kernel(
             if (b, u) == ON_SCALAR:
                 w_tq = held.tile([P, 4, P], BF16, name="w_tq")
                 for t in range(4):
-                    nc.scalar.activation(w_tq[:, t, :], probs[(b, u)][:, t, :], ACT.Copy, scale=vs_t[:, PAGES - 1 - u, t : t + 1])
+                    nc.scalar.activation(w_tq[:, t, :], probs[(b, u)][:, t, :], ACT.Copy, scale=vs_t[:, u, t : t + 1])
                 nc.scalar.copy(w.rearrange("p (c i) t -> p c t i", i=4), w_tq[:].rearrange("p t (c i) -> p c t i", i=4))
             elif (b, u) == ON_GPSIMD:
                 nc.gpsimd.tensor_tensor(
-                    w, probs[(b, u)][:], vs_t[:, PAGES - 1 - u, :].unsqueeze(1).broadcast_to([P, P, 4]), MULT
+                    w, probs[(b, u)][:], vs_t[:, u, :].unsqueeze(1).broadcast_to([P, P, 4]), MULT
                 )
             elif (b, u) == SHARED:
                 nc.gpsimd.tensor_tensor(
                     w[:, 0:GPSIMD_Q], probs[(b, u)][:, 0:GPSIMD_Q],
-                    vs_t[:, PAGES - 1 - u, :].unsqueeze(1).broadcast_to([P, GPSIMD_Q, 4]), MULT,
+                    vs_t[:, u, :].unsqueeze(1).broadcast_to([P, GPSIMD_Q, 4]), MULT,
                 )
                 nc.vector.tensor_tensor(
                     w[:, GPSIMD_Q:P], probs[(b, u)][:, GPSIMD_Q:P],
-                    vs_p[:, PAGES - 1 - u, :].unsqueeze(1).broadcast_to([P, P - GPSIMD_Q, 4]), MULT,
+                    vs_p[u].unsqueeze(1).broadcast_to([P, P - GPSIMD_Q, 4]), MULT,
                 )
             else:
                 nc.vector.tensor_tensor(
-                    w, probs[(b, u)][:], vs_p[:, PAGES - 1 - u, :].unsqueeze(1).broadcast_to([P, P, 4]), MULT
+                    w, probs[(b, u)][:], vs_p[u].unsqueeze(1).broadcast_to([P, P, 4]), MULT
                 )
 
         def quantise(w, b, pages):
@@ -212,7 +221,6 @@ def tile_attend_pkv8q_sigm_kernel(
                 vw_pool[:].rearrange("p u e -> p (u e)").bitcast(U32).indirect(voffs_t[:, lo * vcols : hi * vcols]),
             )
 
-        last = PAGES - 1
         vcols = DV // 16
         early = steps[: QB * last]
         for step in early:

@@ -27,8 +27,8 @@ V_ROW = 4
 VS_ROW = P - 1
 ON_SCALAR = (0, PAGES - 1)
 ON_GPSIMD = (1, 0)
-SHARED = (0, 1)
-GPSIMD_Q = 16
+HOLDS_VALUES = (0, 1)
+SHARED = {(0, 1): 16, (1, PAGES - 1): 28}
 
 
 def tile_attend_pkv8q_sigm_kernel(
@@ -148,7 +148,7 @@ def tile_attend_pkv8q_sigm_kernel(
             if (b, u) == ON_SCALAR:
                 prob = held.tile([P, 4, P], F32, name="prob_tq")
                 nc.scalar.activation(prob[:], score[:], ACT.Sigmoid)
-            elif (b, u) == SHARED:
+            elif (b, u) == HOLDS_VALUES:
                 prob = held.tile([P, P, 4], F32, name="prob_pool", tag="vw_g", align_bytes=64)
                 nc.scalar.activation(prob[:], score[:].rearrange("p t q -> p q t"), ACT.Sigmoid)
             else:
@@ -165,8 +165,8 @@ def tile_attend_pkv8q_sigm_kernel(
         spans = {0: [(0, DV // 2), (DV // 2, DV)], 1: [(0, DV)]}
         acc = {(0, lo): psum.tile([P, hi - lo], F32, name="acc0_%d" % lo) for lo, hi in spans[0]}
         acc[(1, 0)] = psum.tile([P, DV], F32, name="acc1")
-        early_w = [held.tile([P, PAGES - 1, P, 4], BF16, name="early_w%d" % b, align_bytes=64) for b in range(QB)]
-        last_w = [held.tile([P, 1, P, 4], BF16, name="last_w%d" % b, align_bytes=64) for b in range(QB)]
+        early_w = [held.tile([P, PAGES - 1, P, 4], BF16, name="early_w%d" % b, tag="w%d" % b, align_bytes=64) for b in range(QB)]
+        last_w = {}
 
         def weigh(b, u):
             w = early_w[b][:, u] if u < PAGES - 1 else last_w[b][:, 0]
@@ -179,14 +179,15 @@ def tile_attend_pkv8q_sigm_kernel(
                 nc.gpsimd.tensor_tensor(
                     w, probs[(b, u)][:], vs_t[:, u, :].unsqueeze(1).broadcast_to([P, P, 4]), MULT
                 )
-            elif (b, u) == SHARED:
+            elif (b, u) in SHARED:
+                split = SHARED[(b, u)]
                 nc.gpsimd.tensor_tensor(
-                    w[:, 0:GPSIMD_Q], probs[(b, u)][:, 0:GPSIMD_Q],
-                    vs_t[:, u, :].unsqueeze(1).broadcast_to([P, GPSIMD_Q, 4]), MULT,
+                    w[:, 0:split], probs[(b, u)][:, 0:split],
+                    vs_t[:, u, :].unsqueeze(1).broadcast_to([P, split, 4]), MULT,
                 )
                 nc.vector.tensor_tensor(
-                    w[:, GPSIMD_Q:P], probs[(b, u)][:, GPSIMD_Q:P],
-                    vs_p[u].unsqueeze(1).broadcast_to([P, P - GPSIMD_Q, 4]), MULT,
+                    w[:, split:P], probs[(b, u)][:, split:P],
+                    vs_p[u].unsqueeze(1).broadcast_to([P, P - split, 4]), MULT,
                 )
             else:
                 nc.vector.tensor_tensor(
@@ -229,6 +230,8 @@ def tile_attend_pkv8q_sigm_kernel(
         quantise(early_w[0], 0, list(range(last)))
         gather_values(0, last)
         quantise(early_w[1], 1, list(range(last)))
+        last_w[0] = held.tile([P, 1, P, 4], BF16, name="last_w0", align_bytes=64)
+        last_w[1] = held.tile([P, 1, P, 4], BF16, name="last_w1", tag="w1", align_bytes=64)
         weigh(0, last)
         weigh(1, last)
         gather_values(last, PAGES)

@@ -24,6 +24,7 @@ K_HEAD = 4 * T // 32
 VS_FILL = (0, 775, 1552)
 QS_FILL = 33
 V_ROW = 4
+WARM_UP = ([(0, 64)], [(0, 256)], [(0, 128)])
 VS_ROW = P - 1
 ON_SCALAR = (0, PAGES - 1)
 ON_GPSIMD = (1, 0)
@@ -158,6 +159,15 @@ def tile_attend_pkv8q_sigm_kernel(
 
         turned_last = psum.tile([P, 512], F32, name="turned_last", tag="score", bufs=4)
         turn(turned_last, [last])
+        for width in WARM_UP:
+            spare = psum.tile([P, 512], F32, name="spare", tag="score", bufs=4)
+            for lo, hi in width:
+                nc.tensor.matmul_mx(
+                    spare[:, lo:hi],
+                    lhsT=kw_g[:, last, 0, :].bitcast(X4), lhsT_scale=ks_t[:, last, 0, :],
+                    rhs=qw[:, 0 : hi - lo].bitcast(X4), rhs_scale=qs[:, 0 : hi - lo],
+                    start=True, stop=True,
+                )
         for r in range(4):
             nc.sync.dma_start(ks_rows[V_ROW + r : P : 32, 0 : PAGES * DV // 4], vb_g[:].bitcast(I32)[SPREAD * r : P : 32])
 

@@ -21,10 +21,11 @@ MULT = mybir.AluOpType.mult
 
 SPREAD = P // 16
 K_HEAD = 4 * T // 32
-VS_FILL = (0, 775, 1552)
+VS_FILL = (0, 739, 1480)
 QS_FILL = 33
 V_ROW = 4
-WARM_UP = ([(0, 64)], [(0, 256)], [(0, 128)])
+KW_BYTES = 4 * N
+WARM_UP = ([(0, 256)], [(0, 128), (128, 192)])
 VS_ROW = P - 1
 ON_SCALAR = (0, PAGES - 1)
 ON_GPSIMD = (1, 0)
@@ -38,6 +39,7 @@ def tile_attend_pkv8q_sigm_kernel(
     nc = tc.nc
     with ExitStack() as ctx:
         held = ctx.enter_context(tc.tile_pool(name="held", bufs=1))
+        laid = ctx.enter_context(tc.tile_pool(name="laid", bufs=1))
         ring = ctx.enter_context(tc.tile_pool(name="ring", bufs=3))
         psum = ctx.enter_context(tc.psum_pool(name="psum", bufs=1))
 
@@ -46,8 +48,7 @@ def tile_attend_pkv8q_sigm_kernel(
         ks_pool = held.tile([P, T], U8, name="ks_pool", align_bytes=64)
         vs_pool = held.tile([P, T], F32, name="vs_pool", align_bytes=64)
         ident = held.tile([P, P], F32, name="ident", align_bytes=64)
-        zero = held.tile([P, 8], F32, name="zero")
-        half = held.tile([P, 8], F32, name="half")
+        step = held.tile([P, P], F32, name="step", align_bytes=64)
 
         qw = held.tile([P, NQ], I32, name="qw", align_bytes=64)
         qs = held.tile([P, NQ], U8, name="qs", align_bytes=64)
@@ -59,17 +60,16 @@ def tile_attend_pkv8q_sigm_kernel(
         nc.vector.memset(ks_pool[:].bitcast(I32), 0)
         for lo, hi in ((0, QS_FILL), (QS_FILL, NQ // 4)):
             nc.vector.memset(qs[:].bitcast(I32)[:, lo:hi], 0)
-        nc.vector.memset(zero[:, 0:1], 0.0)
         for lo, hi in zip(VS_FILL, VS_FILL[1:]):
             nc.vector.memset(vs_pool[0:VS_ROW, lo:hi], 0.0)
         nc.gpsimd.iota(skew[:], pattern=[[1, P]], base=0, channel_multiplier=-1, allow_small_or_imprecise_dtypes=True)
         nc.gpsimd.memset(vs_pool[0:VS_ROW, VS_FILL[-1] : T], 0.0)
         nc.gpsimd.memset(vb_pool[:].rearrange("p u e -> p (u e)").bitcast(I32), 0)
         nc.scalar.dma_start(vs_pool[VS_ROW:P, :], vs[0:1, :])
-        nc.scalar.activation(half[:, 0:1], zero[:, 0:1], ACT.Sigmoid)
-        dist = held.tile([P, P], F32, name="dist", tag="vs_g", align_bytes=64)
-        nc.scalar.activation(dist[:], skew[:], ACT.Abs, scale=half[:, 0:1])
-        nc.scalar.activation(ident[:], dist[:], ACT.Relu, scale=-4.0, bias=1.0)
+        nc.scalar.activation(step[:], skew[:], ACT.Sigmoid, scale=64.0)
+        dist = laid.tile([P, P], F32, name="dist", offset=KW_BYTES - 1024, align_bytes=64)
+        nc.scalar.activation(dist[:], step[:], ACT.Abs, scale=-2.0, bias=1.0)
+        nc.scalar.activation(ident[:], dist[:], ACT.Relu, scale=-2.0, bias=1.0)
 
         def load_q_scales(r):
             nc.sync.dma_start(qs[r:P:32, :].bitcast(I32), q_scales[0, 0, r:16:4, :].bitcast(I32))
@@ -104,7 +104,7 @@ def tile_attend_pkv8q_sigm_kernel(
             nc.sync.dma_start(ks_rows[r:P:32], ks_rows[SPREAD * r : P : 32])
         last = PAGES - 1
         for u in (0, last):
-            vs_g = held.tile([P, PAGE], F32, name="vs_g%d" % u, tag="vs_g", align_bytes=64)
+            vs_g = laid.tile([P, PAGE], F32, name="vs_g%d" % u, offset=KW_BYTES - (1024 if u == 0 else 0), align_bytes=64)
             nc.scalar.activation(vs_g[:], vs_pool[:].indirect(offs_t[:, u * cols : (u + 1) * cols]), ACT.Copy)
             nc.scalar.copy(vs_d[u][:].rearrange("p t m -> p m t"), vs_g[:].rearrange("p (m t) -> p m t", t=4))
         nc.vector.tensor_copy(
@@ -126,7 +126,7 @@ def tile_attend_pkv8q_sigm_kernel(
         turn(turned, range(last))
         vw_pool = held.tile([P, POOL_PAGES, DV], I32, name="vw_pool", tag="ks_g", align_bytes=64)
         nc.sync.dma_start(vw_pool[:], v_words.rearrange("u p e t -> p u (e t)").bitcast(I32))
-        kw_g = held.tile([P, PAGES, 4, P], U32, name="kw_g", tag="vs_d0", align_bytes=64)
+        kw_g = laid.tile([P, PAGES, 4, P], U32, name="kw_g", offset=0, align_bytes=64)
         for u in range(PAGES):
             nc.vector.tensor_copy(
                 kw_g[:, u].rearrange("p t m -> p m t"),
@@ -159,6 +159,8 @@ def tile_attend_pkv8q_sigm_kernel(
 
         turned_last = psum.tile([P, 512], F32, name="turned_last", tag="score", bufs=4)
         turn(turned_last, [last])
+        halves = [(0, DV // 2), (DV // 2, DV)]
+        acc = {(1, DV // 2): psum.tile([P, DV // 2], F32, name="acc_ring", tag="score", bufs=4)}
         for width in WARM_UP:
             spare = psum.tile([P, 512], F32, name="spare", tag="score", bufs=4)
             for lo, hi in width:
@@ -172,9 +174,8 @@ def tile_attend_pkv8q_sigm_kernel(
             nc.sync.dma_start(ks_rows[V_ROW + r : P : 32, 0 : PAGES * DV // 4], vb_g[:].bitcast(I32)[SPREAD * r : P : 32])
 
         packed = {}
-        spans = {0: [(0, DV // 2), (DV // 2, DV)], 1: [(0, DV)]}
-        acc = {(0, lo): psum.tile([P, hi - lo], F32, name="acc0_%d" % lo) for lo, hi in spans[0]}
-        acc[(1, 0)] = psum.tile([P, DV], F32, name="acc1")
+        for b, lo in ((0, 0), (0, DV // 2), (1, 0)):
+            acc[(b, lo)] = psum.tile([P, DV // 2], F32, name="acc%d_%d" % (b, lo))
         early_w = [held.tile([P, PAGES - 1, P, 4], BF16, name="early_w%d" % b, tag="w%d" % b, align_bytes=64) for b in range(QB)]
         last_w = {}
 
@@ -217,7 +218,7 @@ def tile_attend_pkv8q_sigm_kernel(
 
         def multiply(b, u):
             codes, plane = packed[(b, u)]
-            for lo, hi in spans[b]:
+            for lo, hi in halves:
                 ecols = slice(u * DV + lo, u * DV + hi)
                 nc.tensor.matmul_mx(
                     acc[(b, lo)][:],
@@ -250,10 +251,11 @@ def tile_attend_pkv8q_sigm_kernel(
         for b, u in sorted(early) + [(1, last), (0, last)]:
             multiply(b, u)
         for b in reversed(range(QB)):
-            for lo, hi in spans[b]:
-                res = held.tile([P, hi - lo], F32, name="res%d_%d" % (b, lo))
+            res = held.tile([P, DV], F32, name="res%d" % b, align_bytes=64)
+            for lo, hi in halves:
                 if lo == 0:
-                    nc.vector.tensor_scalar_mul(res[:], acc[(b, lo)][:], 1.0 / 16.0)
+                    nc.vector.tensor_scalar_mul(res[:, lo:hi], acc[(b, lo)][:], 1.0 / 16.0)
                 else:
-                    nc.scalar.activation(res[:], acc[(b, lo)][:], ACT.Copy, scale=1.0 / 16.0)
-                nc.sync.dma_start(out[0, b * P : (b + 1) * P, lo:hi], res[:])
+                    nc.scalar.activation(res[:, lo:hi], acc[(b, lo)][:], ACT.Copy, scale=1.0 / 16.0)
+            for lo, hi in halves if b == 0 else [(0, DV)]:
+                nc.sync.dma_start(out[0, b * P : (b + 1) * P, lo:hi], res[:, lo:hi])

@@ -25,7 +25,7 @@ VS_FILL = (0, 739, 1480)
 QS_FILL = 33
 V_ROW = 4
 KW_BYTES = 4 * N
-WARM_UP = ([(0, 256)], [(0, 128), (128, 192)])
+WARM_UP = ((0, 256), (256, 384), (384, 448))
 VS_ROW = P - 1
 ON_SCALAR = (0, PAGES - 1)
 ON_GPSIMD = (1, 0)
@@ -160,22 +160,21 @@ def tile_attend_pkv8q_sigm_kernel(
         turned_last = psum.tile([P, 512], F32, name="turned_last", tag="score", bufs=4)
         turn(turned_last, [last])
         halves = [(0, DV // 2), (DV // 2, DV)]
-        acc = {(1, DV // 2): psum.tile([P, DV // 2], F32, name="acc_ring", tag="score", bufs=4)}
-        for width in WARM_UP:
-            spare = psum.tile([P, 512], F32, name="spare", tag="score", bufs=4)
-            for lo, hi in width:
-                nc.tensor.matmul_mx(
-                    spare[:, lo:hi],
-                    lhsT=kw_g[:, last, 0, :].bitcast(X4), lhsT_scale=ks_t[:, last, 0, :],
-                    rhs=qw[:, 0 : hi - lo].bitcast(X4), rhs_scale=qs[:, 0 : hi - lo],
-                    start=True, stop=True,
-                )
+        acc = {(1, lo): psum.tile([P, hi - lo], F32, name="acc1_%d" % lo, tag="score", bufs=4) for lo, hi in halves}
+        spare = psum.tile([P, 512], F32, name="spare", tag="score", bufs=4)
+        for lo, hi in WARM_UP:
+            nc.tensor.matmul_mx(
+                spare[:, lo:hi],
+                lhsT=kw_g[:, last, 0, :].bitcast(X4), lhsT_scale=ks_t[:, last, 0, :],
+                rhs=qw[:, 0 : hi - lo].bitcast(X4), rhs_scale=qs[:, 0 : hi - lo],
+                start=True, stop=True,
+            )
         for r in range(4):
             nc.sync.dma_start(ks_rows[V_ROW + r : P : 32, 0 : PAGES * DV // 4], vb_g[:].bitcast(I32)[SPREAD * r : P : 32])
 
         packed = {}
-        for b, lo in ((0, 0), (0, DV // 2), (1, 0)):
-            acc[(b, lo)] = psum.tile([P, DV // 2], F32, name="acc%d_%d" % (b, lo))
+        for lo, hi in halves:
+            acc[(0, lo)] = psum.tile([P, hi - lo], F32, name="acc0_%d" % lo)
         early_w = [held.tile([P, PAGES - 1, P, 4], BF16, name="early_w%d" % b, tag="w%d" % b, align_bytes=64) for b in range(QB)]
         last_w = {}
 

from contextlib import ExitStack

import concourse.mybir as mybir

N, T, D, DV, NQ, PAGE = 1536, 4096, 512, 256, 256, 512
P = 128
PAGES = N // PAGE
POOL_PAGES = T // PAGE
QB = NQ // P
FLOPS = 2 * NQ * N * (D + DV)

F32 = mybir.dt.float32
BF16 = mybir.dt.bfloat16
I32 = mybir.dt.int32
U32 = mybir.dt.uint32
U16 = mybir.dt.uint16
U8 = mybir.dt.uint8
X4 = mybir.dt.float8_e4m3fn_x4
ACT = mybir.ActivationFunctionType
MULT = mybir.AluOpType.mult

SPREAD = P // 16
K_HEAD = 4 * T // 32
VS_FILL = (0, 739, 1480)
QS_FILL = 33
V_ROW = 4
KW_BYTES = 4 * N
WARM_UP = ((0, 256), (256, 384), (384, 448))
VS_ROW = P - 1
ON_SCALAR = (0, PAGES - 1)
ON_GPSIMD = (1, 0)
HOLDS_VALUES = (0, 1)
SHARED = {(0, 1): 16, (1, PAGES - 1): 28}


def tile_attend_pkv8q_sigm_kernel(
    tc, q_words, q_scales, k_words, k_scales, v_words, v_scales, vs, offs, voffs, out
):
    nc = tc.nc
    with ExitStack() as ctx:
        held = ctx.enter_context(tc.tile_pool(name="held", bufs=1))
        laid = ctx.enter_context(tc.tile_pool(name="laid", bufs=1))
        ring = ctx.enter_context(tc.tile_pool(name="ring", bufs=3))
        psum = ctx.enter_context(tc.psum_pool(name="psum", bufs=1))

        offs_t = held.tile([P, N // 16], U16, name="offs_t")
        voffs_t = held.tile([P, PAGES * DV // 16], U16, name="voffs_t")
        ks_pool = held.tile([P, T], U8, name="ks_pool", align_bytes=64)
        vs_pool = held.tile([P, T], F32, name="vs_pool", align_bytes=64)
        ident = held.tile([P, P], F32, name="ident", align_bytes=64)
        step = held.tile([P, P], F32, name="step", align_bytes=64)

        qw = held.tile([P, NQ], I32, name="qw", align_bytes=64)
        qs = held.tile([P, NQ], U8, name="qs", align_bytes=64)
        kw_pool = held.tile([P, T], I32, name="kw_pool", align_bytes=64)

        vb_pool = held.tile([P, POOL_PAGES, DV], U8, name="vb_pool", align_bytes=64)
        skew = held.tile([P, P], F32, name="skew", align_bytes=64)

        nc.vector.memset(ks_pool[:].bitcast(I32), 0)
        for lo, hi in ((0, QS_FILL), (QS_FILL, NQ // 4)):
            nc.vector.memset(qs[:].bitcast(I32)[:, lo:hi], 0)
        for lo, hi in zip(VS_FILL, VS_FILL[1:]):
            nc.vector.memset(vs_pool[0:VS_ROW, lo:hi], 0.0)
        nc.gpsimd.iota(skew[:], pattern=[[1, P]], base=0, channel_multiplier=-1, allow_small_or_imprecise_dtypes=True)
        nc.gpsimd.memset(vs_pool[0:VS_ROW, VS_FILL[-1] : T], 0.0)
        nc.gpsimd.memset(vb_pool[:].rearrange("p u e -> p (u e)").bitcast(I32), 0)
        nc.scalar.dma_start(vs_pool[VS_ROW:P, :], vs[0:1, :])
        nc.scalar.activation(step[:], skew[:], ACT.Sigmoid, scale=64.0)
        dist = laid.tile([P, P], F32, name="dist", offset=KW_BYTES - 1024, align_bytes=64)
        nc.scalar.activation(dist[:], step[:], ACT.Abs, scale=-2.0, bias=1.0)
        nc.scalar.activation(ident[:], dist[:], ACT.Relu, scale=-2.0, bias=1.0)

        def load_q_scales(r):
            nc.sync.dma_start(qs[r:P:32, :].bitcast(I32), q_scales[0, 0, r:16:4, :].bitcast(I32))

        k_flat = k_words[0].rearrange("p n t -> p (n t)").bitcast(I32)
        nc.sync.dma_start(offs_t[:], offs)
        nc.sync.dma_start(kw_pool[:, 0:K_HEAD], k_flat[:, 0:K_HEAD])
        nc.sync.dma_start(voffs_t[:], voffs)
        nc.sync.dma_start(ks_pool[0:P:SPREAD, :].bitcast(I32), k_scales[0].bitcast(I32))
        for r in range(2):
            load_q_scales(r)
        nc.sync.dma_start(kw_pool[:, K_HEAD:T], k_flat[:, K_HEAD:T])
        nc.sync.dma_start(qw[:], q_words[0, 0].rearrange("p n t -> p (n t)").bitcast(I32))
        for r in range(2, 4):
            load_q_scales(r)
        nc.sync.dma_start(vb_pool[0:P:SPREAD].bitcast(I32), v_scales.rearrange("u f e -> f u e").bitcast(I32))

        cols = PAGE // 16
        ks_g = held.tile([P, N], U8, name="ks_g", tag="ks_g", align_bytes=64)
        ks_t = held.tile([P, PAGES, 4, P], U8, name="ks_t", align_bytes=64)
        vs_d = [held.tile([P, 4, P], F32, name="vs_d%d" % u, tag="vs_d%d" % u, align_bytes=64) for u in range(PAGES)]
        vb_g = held.tile([P, PAGES * DV], U8, name="vb_g", align_bytes=64)
        turned = psum.tile([P, 512], F32, name="turned")
        for lo, hi in ((0, PAGES - 1), (PAGES - 1, PAGES)):
            nc.vector.tensor_copy(ks_g[:, lo * PAGE : hi * PAGE], ks_pool[:].indirect(offs_t[:, lo * cols : hi * cols]))
        for lo, hi in ((0, PAGES - 1), (PAGES - 1, PAGES)):
            nc.vector.tensor_copy(
                ks_t[:, lo:hi], ks_g[:, lo * PAGE : hi * PAGE].rearrange("p (u m t) -> p u t m", u=hi - lo, t=4)
            )
        ks_rows = ks_t[:].rearrange("p u t m -> p (u t m)").bitcast(I32)
        for r in range(1, 4):
            nc.sync.dma_start(ks_rows[r:P:32], ks_rows[SPREAD * r : P : 32])
        last = PAGES - 1
        for u in (0, last):
            vs_g = laid.tile([P, PAGE], F32, name="vs_g%d" % u, offset=KW_BYTES - (1024 if u == 0 else 0), align_bytes=64)
            nc.scalar.activation(vs_g[:], vs_pool[:].indirect(offs_t[:, u * cols : (u + 1) * cols]), ACT.Copy)
            nc.scalar.copy(vs_d[u][:].rearrange("p t m -> p m t"), vs_g[:].rearrange("p (m t) -> p m t", t=4))
        nc.vector.tensor_copy(
            vs_d[1][:].bitcast(U32).rearrange("p t m -> p m t"),
            vs_pool[:].bitcast(U32).indirect(offs_t[:, cols : 2 * cols]),
        )
        vs_t = held.tile([P, PAGES, 4], F32, name="vs_t", align_bytes=64)
        vs_p = {}

        def turn(bank, pages):
            for i, u in enumerate(pages):
                base = 1 + 4 * (len(pages) - 1 - i)
                for t in reversed(range(4)):
                    nc.tensor.transpose(bank[:, base + t : base + t + P], vs_d[u][:, t, :], ident[:])
                vs_p[u] = bank[:, base + VS_ROW : base + VS_ROW + 4]
            for u in pages:
                nc.scalar.copy(vs_t[:, u], vs_p[u])

        turn(turned, range(last))
        vw_pool = held.tile([P, POOL_PAGES, DV], I32, name="vw_pool", tag="ks_g", align_bytes=64)
        nc.sync.dma_start(vw_pool[:], v_words.rearrange("u p e t -> p u (e t)").bitcast(I32))
        kw_g = laid.tile([P, PAGES, 4, P], U32, name="kw_g", offset=0, align_bytes=64)
        for u in range(PAGES):
            nc.vector.tensor_copy(
                kw_g[:, u].rearrange("p t m -> p m t"),
                kw_pool[:].bitcast(U32).indirect(offs_t[:, u * cols : (u + 1) * cols]),
            )
        nc.vector.tensor_copy(vb_g[:], vb_pool[:].rearrange("p u e -> p (u e)").indirect(voffs_t[:]))

        steps = [(b, u) for u in range(PAGES) for b in range(QB)]
        probs = {}
        for b, u in steps:
            score = psum.tile([P, 4, P], F32, name="score", tag="score", bufs=4)
            qcols = slice(b * P, (b + 1) * P)
            for t in range(4):
                nc.tensor.matmul_mx(
                    score[:, t, :],
                    lhsT=kw_g[:, u, t, :].bitcast(X4), lhsT_scale=ks_t[:, u, t, :],
                    rhs=qw[:, qcols].bitcast(X4), rhs_scale=qs[:, qcols],
                    start=True, stop=True,
                )
            if (b, u) == ON_SCALAR:
                prob = held.tile([P, 4, P], F32, name="prob_tq")
                nc.scalar.activation(prob[:], score[:], ACT.Sigmoid)
            elif (b, u) == HOLDS_VALUES:
                prob = held.tile([P, P, 4], F32, name="prob_pool", tag="vw_g", align_bytes=64)
                nc.scalar.activation(prob[:], score[:].rearrange("p t q -> p q t"), ACT.Sigmoid)
            else:
                prob = ring.tile([P, P, 4], F32, name="prob", bufs=5)
                nc.scalar.activation(prob[:], score[:].rearrange("p t q -> p q t"), ACT.Sigmoid)
            probs[(b, u)] = prob

        turned_last = psum.tile([P, 512], F32, name="turned_last", tag="score", bufs=4)
        turn(turned_last, [last])
        halves = [(0, DV // 2), (DV // 2, DV)]
        acc = {(1, lo): psum.tile([P, hi - lo], F32, name="acc1_%d" % lo, tag="score", bufs=4) for lo, hi in halves}
        spare = psum.tile([P, 512], F32, name="spare", tag="score", bufs=4)
        for lo, hi in WARM_UP:
            nc.tensor.matmul_mx(
                spare[:, lo:hi],
                lhsT=kw_g[:, last, 0, :].bitcast(X4), lhsT_scale=ks_t[:, last, 0, :],
                rhs=qw[:, 0 : hi - lo].bitcast(X4), rhs_scale=qs[:, 0 : hi - lo],
                start=True, stop=True,
            )
        for r in range(4):
            nc.sync.dma_start(ks_rows[V_ROW + r : P : 32, 0 : PAGES * DV // 4], vb_g[:].bitcast(I32)[SPREAD * r : P : 32])

        packed = {}
        for lo, hi in halves:
            acc[(0, lo)] = psum.tile([P, hi - lo], F32, name="acc0_%d" % lo)
        early_w = [held.tile([P, PAGES - 1, P, 4], BF16, name="early_w%d" % b, tag="w%d" % b, align_bytes=64) for b in range(QB)]
        last_w = {}

        def weigh(b, u):
            w = early_w[b][:, u] if u < PAGES - 1 else last_w[b][:, 0]
            if (b, u) == ON_SCALAR:
                w_tq = held.tile([P, 4, P], BF16, name="w_tq")
                for t in range(4):
                    nc.scalar.activation(w_tq[:, t, :], probs[(b, u)][:, t, :], ACT.Copy, scale=vs_t[:, u, t : t + 1])
                nc.scalar.copy(w.rearrange("p (c i) t -> p c t i", i=4), w_tq[:].rearrange("p t (c i) -> p c t i", i=4))
            elif (b, u) == ON_GPSIMD:
                nc.gpsimd.tensor_tensor(
                    w, probs[(b, u)][:], vs_t[:, u, :].unsqueeze(1).broadcast_to([P, P, 4]), MULT
                )
            elif (b, u) in SHARED:
                split = SHARED[(b, u)]
                nc.gpsimd.tensor_tensor(
                    w[:, 0:split], probs[(b, u)][:, 0:split],
                    vs_t[:, u, :].unsqueeze(1).broadcast_to([P, split, 4]), MULT,
                )
                nc.vector.tensor_tensor(
                    w[:, split:P], probs[(b, u)][:, split:P],
                    vs_p[u].unsqueeze(1).broadcast_to([P, P - split, 4]), MULT,
                )
            else:
                nc.vector.tensor_tensor(
                    w, probs[(b, u)][:], vs_p[u].unsqueeze(1).broadcast_to([P, P, 4]), MULT
                )

        def quantise(w, b, pages):
            codes = held.tile([P, len(pages), P], U32, name="codes%d_%d" % (b, pages[0]), align_bytes=64)
            plane = held.tile([P, len(pages), P], U8, name="plane%d_%d" % (b, pages[0]), align_bytes=64)
            nc.vector.quantize_mx(
                codes[:].rearrange("p u q -> p (u q)").bitcast(X4),
                plane[:].rearrange("p u q -> p (u q)"),
                w[:].rearrange("p u q t -> p (u q t)"),
            )
            for i, u in enumerate(pages):
                packed[(b, u)] = (codes[:, i], plane[:, i])

        def multiply(b, u):
            codes, plane = packed[(b, u)]
            for lo, hi in halves:
                ecols = slice(u * DV + lo, u * DV + hi)
                nc.tensor.matmul_mx(
                    acc[(b, lo)][:],
                    lhsT=codes.bitcast(X4), lhsT_scale=plane,
                    rhs=vw_g[:, ecols].bitcast(X4), rhs_scale=ks_t[:].rearrange("p u t m -> p (u t m)")[V_ROW:P, ecols],
                    start=(u == 0), stop=(u == PAGES - 1),
                )

        def gather_values(lo, hi):
            nc.vector.tensor_copy(
                vw_g[:, lo * DV : hi * DV],
                vw_pool[:].rearrange("p u e -> p (u e)").bitcast(U32).indirect(voffs_t[:, lo * vcols : hi * vcols]),
            )

        vcols = DV // 16
        early = steps[: QB * last]
        for step in early:
            weigh(*step)
        vw_g = held.tile([P, PAGES * DV], U32, name="vw_g", tag="vw_g", align_bytes=64)
        quantise(early_w[0], 0, list(range(last)))
        gather_values(0, last)
        quantise(early_w[1], 1, list(range(last)))
        last_w[0] = held.tile([P, 1, P, 4], BF16, name="last_w0", align_bytes=64)
        last_w[1] = held.tile([P, 1, P, 4], BF16, name="last_w1", tag="w1", align_bytes=64)
        weigh(0, last)
        weigh(1, last)
        gather_values(last, PAGES)
        quantise(last_w[1], 1, [last])
        quantise(last_w[0], 0, [last])
        for b, u in sorted(early) + [(1, last), (0, last)]:
            multiply(b, u)
        for b in reversed(range(QB)):
            res = held.tile([P, DV], F32, name="res%d" % b, align_bytes=64)
            for lo, hi in halves:
                if lo == 0:
                    nc.vector.tensor_scalar_mul(res[:, lo:hi], acc[(b, lo)][:], 1.0 / 16.0)
                else:
                    nc.scalar.activation(res[:, lo:hi], acc[(b, lo)][:], ACT.Copy, scale=1.0 / 16.0)
            for lo, hi in halves if b == 0 else [(0, DV)]:
                nc.sync.dma_start(out[0, b * P : (b + 1) * P, lo:hi], res[:, lo:hi])
